import numpy as np
import ml_dtypes


def mxq(x, axis, fmt="e4m3"):
    dtype, down = {"e4m3": (ml_dtypes.float8_e4m3fn, 7), "e5m2": (ml_dtypes.float8_e5m2, 14)}[fmt]
    v = np.moveaxis(np.asarray(x, np.float32).astype(ml_dtypes.bfloat16).astype(np.float64), axis, -1)
    blocks = v.reshape(v.shape[:-1] + (-1, 32))
    amax = np.abs(blocks).max(-1, keepdims=True)
    byte = np.maximum(np.where(amax > 0, np.frexp(amax)[1] - 1 + 127, 0) - down, 1)
    scale = np.exp2(byte - 127.0)
    codes = (blocks / scale).astype(np.float32).astype(dtype).astype(np.float64)
    return np.moveaxis((codes * scale).reshape(v.shape), -1, axis)


WIDE = False


def mx_kscale(k):
    if not WIDE:
        return np.ones(k)
    levels = np.array([10, -10, 5, -5, 0])
    if k % 512:
        return np.exp2(np.random.permutation(np.resize(levels, k // 32))).repeat(32)
    a = np.empty((k // 512, 16))
    for p in range(k // 512):
        a[p, :8] = np.random.permutation(np.resize(levels, 8))
        for g in range(8):
            far = levels[np.abs(levels - a[p, g]) >= 10]
            a[p, g + 8] = far[np.random.randint(len(far))]
    return np.exp2(a.ravel()).repeat(32)


def f64(x):
    return np.asarray(x).astype(np.float64)


def striped(idx):
    return np.tile(idx.reshape(-1, 16).T, (8, 1)).astype(np.uint16)


def unstriped(offs):
    return offs[:16].T.reshape(-1).astype(np.int64)


E2M1 = np.array([0.0, 0.5, 1.0, 1.5, 2.0, 3.0, 4.0, 6.0, -0.0, -0.5, -1.0, -1.5, -2.0, -3.0, -4.0, -6.0])


def pack_weight(w, fmt):
    k, n = w.shape
    w = f64(np.asarray(w, np.float32).astype(ml_dtypes.bfloat16)).reshape(k // 32, 32, n)
    amax = np.abs(w).max(1)
    if fmt == "e4m3":
        byte = np.frexp(amax)[1] - 1 + 127 - 7
    else:
        mant, ex = np.frexp(amax / 6.0)
        byte = np.where(mant > 0.5, ex, ex - 1) + 127
    byte = np.clip(np.where(amax > 0, byte, 1), 1, 254)
    scaled = (w * np.exp2(127.0 - byte)[:, None, :]).reshape(k, n).astype(np.float32)
    by_word = np.ascontiguousarray(scaled.reshape(k // 512, 128, 4, n).transpose(0, 1, 3, 2))
    if fmt == "e4m3":
        words = by_word.astype(ml_dtypes.float8_e4m3fn).view(np.uint8)
    else:
        c = by_word.astype(ml_dtypes.float4_e2m1fn).view(np.uint8) & 0xF
        words = (c[..., 0::2] | (c[..., 1::2] << 4)).reshape(k // 512, 128, 2 * n)
    return np.ascontiguousarray(words), np.ascontiguousarray(byte.astype(np.uint8).reshape(k // 512, 16, n))


def unpack_weight(words, scales, fmt):
    g, _, n = scales.shape
    words = np.ascontiguousarray(words).reshape(g, 128, n, -1)
    if fmt == "e4m3":
        vals = words.view(ml_dtypes.float8_e4m3fn).astype(np.float64)
    else:
        nib = np.empty((g, 128, n, 4), np.uint8)
        nib[..., 0::2] = words & 0xF
        nib[..., 1::2] = words >> 4
        vals = E2M1[nib]
    vals = vals * np.repeat(np.exp2(scales.astype(np.float64) - 127.0), 8, axis=1)[..., None]
    return vals.transpose(0, 1, 3, 2).reshape(g * 512, n)


def gelu(v):
    return 0.5 * v * (1.0 + np.tanh(np.sqrt(2.0 / np.pi) * (v + 0.044715 * v**3)))


def bf(x):
    return np.asarray(x, np.float32).astype(ml_dtypes.bfloat16)


def planes(Y):
    n, m = Y.shape
    b = f64(bf(Y)).reshape(n // 32, 32, m)
    amax = np.abs(b).max(1)
    byte = np.clip(np.where(amax > 0, np.frexp(amax)[1] - 1 + 127 - 7, 1), 1, 254)
    codes = (b * np.exp2(127.0 - byte)[:, None, :]).reshape(n, m).astype(np.float32).astype(ml_dtypes.float8_e4m3fn).view(np.uint8)
    words = codes.reshape(n // 512, 128, 4, m).transpose(0, 1, 3, 2)
    return np.ascontiguousarray(words), np.ascontiguousarray(byte.astype(np.uint8).reshape(n // 512, 16, m))


K, T, S, T2, H, N = 1024, 4096, 1024, 2048, 512, 512

def setup_inputs():
    n = np.random.standard_normal
    s = mx_kscale(K)[:, None]
    u = mx_kscale(H)[:, None]
    tab_words, tab_scales = pack_weight(n((K, T)) * s, "e4m3")
    wb_words, wb_scales = pack_weight(n((H, N)) / np.sqrt(H) / u, "e2m1")
    return {
        "tab_words": tab_words, "tab_scales": tab_scales,
        "offs": striped(np.random.permutation(T)[:S]),
        "w1": (0.6 * n((K, H)) / np.sqrt(K) / s).astype(np.float32),
        "gain": (np.random.uniform(0.7, 1.8, H) * u[:, 0]).astype(np.float32),
        "page0": (n((H, T2)) * u).astype(np.float32),
        "offs2": striped(np.random.permutation(T2)[:S]),
        "wgs": np.exp(0.3 * n((128, S))).astype(np.float32),
        "wa": (n((H, N)) / np.sqrt(H) / u).astype(np.float32),
        "wb_words": wb_words, "wb_scales": wb_scales,
    }

def reference(tab_words, tab_scales, offs, w1, gain, page0, offs2, wgs, wa, wb_words, wb_scales):
    v = unpack_weight(tab_words, tab_scales, "e4m3")[:, unstriped(offs)]
    q = mxq(f64(w1), 0, "e4m3").T @ v
    h = f64(gain)[:, None] * np.exp(-np.square(q))
    page = f64(page0).copy()
    page[:, unstriped(offs2)] = np.tile(f64(wgs), (H // 128, 1)) * h
    words, scales = planes(page)
    pq = mxq(page, 0, "e4m3")
    a = mxq(f64(wa), 0, "e4m3").T @ pq
    b = unpack_weight(wb_words, wb_scales, "e2m1").T @ pq
    y = np.tanh(a) + b
    return y, page, words, scales

@@ -1,0 +1,241 @@
+from contextlib import ExitStack
+
+import concourse.mybir as mybir
+
+K, T, S, T2, H, N = 1024, 4096, 1024, 2048, 512, 512
+FLOPS = 2 * K * H * S + 2 * 2 * H * N * T2
+
+F32 = mybir.dt.float32
+BF16 = mybir.dt.bfloat16
+I32 = mybir.dt.int32
+U32 = mybir.dt.uint32
+U16 = mybir.dt.uint16
+U8 = mybir.dt.uint8
+FP8X4 = mybir.dt.float8_e4m3fn_x4
+FP4X4 = mybir.dt.float4_e2m1fn_x4
+ACT = mybir.ActivationFunctionType
+ALU = mybir.AluOpType
+
+P = 128
+PACK = 4
+QUAD = 32
+BANK = 512
+PASSES = K // (P * PACK)
+HALVES = S // BANK
+CHUNKS = T2 // BANK
+LIST_COLS = BANK // 16
+Y_BUFS = 10
+
+
+def tile_list_allergy_archive_kernel(
+    tc, tab_words, tab_scales, offs, w1, gain, page0, offs2, wgs, wa, wb_words, wb_scales,
+    out_0, out_1, out_2, out_3,
+):
+    nc = tc.nc
+    with ExitStack() as ctx:
+        lists = ctx.enter_context(tc.tile_pool(name="lists", bufs=1))
+        keep = ctx.enter_context(tc.tile_pool(name="keep", bufs=1))
+        shared = ctx.enter_context(tc.tile_pool(name="shared", bufs=1))
+        ring = ctx.enter_context(tc.tile_pool(name="ring", bufs=Y_BUFS))
+        psum = ctx.enter_context(tc.psum_pool(name="psum", bufs=1))
+
+        def held(name, shape, dtype):
+            return keep.tile(shape, dtype, name=name, tag=name, align_bytes=64)
+
+        def bank(i):
+            return psum.tile([P, BANK], F32, name="bank%d" % i)
+
+        pick = lists.tile([P, S // 16], U16, name="pick")
+        place = lists.tile([P, S // 16], U16, name="place")
+
+        tab_plane = held("tab_plane", [P, T], U8)
+        wb_plane = held("wb_plane", [P, N], U8)
+        nc.vector.memset(tab_plane[:].bitcast(I32), 0)
+        nc.vector.memset(wb_plane[:].bitcast(I32), 0)
+        for q in range(4):
+            nc.gpsimd.dma_start(
+                out=tab_plane[QUAD * q : QUAD * q + 4 * PASSES, :].bitcast(I32),
+                in_=tab_scales[:, 4 * q : 4 * q + 4, :].bitcast(I32),
+            )
+        for q in range(4):
+            nc.gpsimd.dma_start(
+                out=wb_plane[QUAD * q : QUAD * q + 4, :].bitcast(I32),
+                in_=wb_scales[0, 4 * q : 4 * q + 4, :].bitcast(I32),
+            )
+
+        nc.sync.dma_start(pick[:], offs)
+        w1_raw, tab = [], []
+        for a in range(PASSES):
+            w1_raw.append(held("w1_raw%d" % a, [P, PACK, H], F32))
+            nc.sync.dma_start(
+                out=w1_raw[a][:],
+                in_=w1[a * P * PACK : (a + 1) * P * PACK, :].rearrange("(p j) c -> p j c", j=PACK),
+            )
+            tab.append(held("tab%d" % a, [P, T], U32))
+            nc.sync.dma_start(
+                out=tab[a][:].bitcast(I32),
+                in_=tab_words[a].rearrange("p n t -> p (n t)").bitcast(I32),
+            )
+        nc.sync.dma_start(place[:], offs2)
+        gain_sb = held("gain_sb", [P, PACK], F32)
+        nc.sync.dma_start(out=gain_sb[:], in_=gain.rearrange("(p t) -> p t", t=PACK))
+
+        wgs_rows = wgs.rearrange("(p t) j -> p (t j)", t=PACK)
+        page_rows = page0.rearrange("(p t) m -> t p m", t=PACK)
+        page = [held("page%d" % t, [P, T2], F32) for t in range(PACK)]
+        wgs_sb = held("wgs_sb", [P, PACK * S], F32)
+        early = shared.tile([P, PACK * S + PACK * N], F32, name="early", offset=0)
+        squares = early[:, : PACK * S]
+        wa_raw = early[:, PACK * S :]
+
+        def load_wgs(lo, hi):
+            for q in (0, 2, 1, 3):
+                nc.sync.dma_start(out=wgs_sb[QUAD * q : QUAD * (q + 1), lo:hi], in_=wgs_rows[:, lo:hi])
+
+        halves = [slice(h * BANK, (h + 1) * BANK) for h in range(HALVES)]
+        load_wgs(0, BANK)
+        nc.sync.dma_start(out=page[0][:], in_=page_rows[0])
+        load_wgs(BANK, 2 * S)
+        nc.sync.dma_start(out=page[1][:], in_=page_rows[1])
+        load_wgs(2 * S, 4 * S)
+        nc.sync.dma_start(out=wa_raw, in_=wa.rearrange("(p j) n -> p (j n)", j=PACK))
+        nc.sync.dma_start(out=page[2][:], in_=page_rows[2])
+        nc.sync.dma_start(out=page[3][:], in_=page_rows[3])
+        wb_codes = held("wb_codes", [P, 2 * N], U8)
+        nc.sync.dma_start(out=wb_codes[:].bitcast(I32), in_=wb_words[0].bitcast(I32))
+
+        picked_plane = held("picked_plane", [P, S], U8)
+        nc.vector.tensor_copy(picked_plane[:], tab_plane[:].indirect(pick[:]))
+
+        w1_codes, w1_plane, picked = [], [], []
+        for a in range(PASSES):
+            w1_bf = held("w1_bf%d" % a, [P, PACK * H], BF16)
+            nc.scalar.activation(
+                out=w1_bf[:].rearrange("p (t m j) -> p m j t", t=PACK, j=PACK),
+                in_=w1_raw[a][:].rearrange("p j (m t) -> p m j t", t=PACK),
+                func=ACT.Copy,
+            )
+            w1_codes.append(held("w1_codes%d" % a, [P, H], U32))
+            w1_plane.append(held("w1_plane%d" % a, [P, H], U8))
+            nc.vector.quantize_mx(out=w1_codes[a][:].bitcast(FP8X4), scales=w1_plane[a][:], in_=w1_bf[:])
+            picked.append([held("picked%d_%d" % (a, h), [P, BANK], U32) for h in range(HALVES)])
+            for h in range(HALVES):
+                nc.vector.tensor_copy(
+                    picked[a][h][:], tab[a][:].indirect(pick[:, h * LIST_COLS : (h + 1) * LIST_COLS])
+                )
+
+        q_bank = [[bank(HALVES * t + h) for h in range(HALVES)] for t in range(PACK)]
+        for a in range(PASSES):
+            for h in range(HALVES):
+                for t in range(PACK):
+                    rows = slice(t * P, (t + 1) * P)
+                    nc.tensor.matmul_mx(
+                        out=q_bank[t][h][:],
+                        lhsT=w1_codes[a][:, rows].bitcast(FP8X4),
+                        lhsT_scale=w1_plane[a][:, rows],
+                        rhs=picked[a][h][:].bitcast(FP8X4),
+                        rhs_scale=picked_plane[4 * a :, halves[h]],
+                        start=(a == 0),
+                        stop=(a == PASSES - 1),
+                    )
+
+        feature = [held("feature%d" % t, [P, S], F32) for t in range(PACK)]
+        pieces = [halves] + [[slice(0, S)]] * (PACK - 1)
+        wgs_gain = held("wgs_gain", [P, BANK], F32)
+        nc.scalar.activation(out=wgs_gain[:], in_=wgs_sb[:, :BANK], func=ACT.Copy, scale=gain_sb[:, 0:1])
+        factor = {}
+        for t in range(PACK):
+            for cols in pieces[t]:
+                wide = slice(t * S + cols.start, t * S + cols.stop)
+                for h in range(cols.start // BANK, cols.stop // BANK):
+                    nc.scalar.activation(
+                        out=squares[:, t * S + h * BANK : t * S + (h + 1) * BANK], in_=q_bank[t][h][:], func=ACT.Square
+                    )
+                nc.scalar.activation(out=feature[t][:, cols], in_=squares[:, wide], func=ACT.Exp, scale=-1.0)
+                if wide.start == 0:
+                    factor[wide.start] = wgs_gain[:]
+                else:
+                    factor[wide.start] = wgs_sb[:, wide]
+                    nc.scalar.activation(
+                        out=feature[t][:, cols], in_=feature[t][:, cols], func=ACT.Copy, scale=gain_sb[:, t : t + 1]
+                    )
+
+        wa_bf = held("wa_bf", [P, N * PACK], BF16)
+        nc.scalar.activation(
+            out=wa_bf[:].rearrange("p (c i j) -> p c j i", i=4, j=PACK),
+            in_=wa_raw.rearrange("p (j c i) -> p c j i", i=4, j=PACK),
+            func=ACT.Copy,
+        )
+
+        out_1_rows = out_1.rearrange("(p t) m -> t p m", t=PACK)
+        chunks = [slice(c * BANK, (c + 1) * BANK) for c in range(CHUNKS)]
+        pairs = [
+            shared.tile([P, 2, BANK, 2], BF16, name="pairs%d" % c, offset=c * BANK * PACK * 2)
+            for c in range(CHUNKS)
+        ]
+
+        def round_into_pairs(t, c):
+            nc.scalar.activation(out=pairs[c][:, t // 2, :, t % 2], in_=page[t][:, chunks[c]], func=ACT.Copy)
+
+        for t in range(PACK):
+            for cols in pieces[t]:
+                nc.vector.tensor_tensor(
+                    page[t][:].indirect(place[:, cols.start // 16 : cols.stop // 16]),
+                    feature[t][:, cols],
+                    factor[t * S + cols.start],
+                    ALU.mult,
+                )
+            nc.sync.dma_start(out=out_1_rows[t], in_=page[t][:])
+            if t < PACK - 1:
+                for c in range(CHUNKS):
+                    round_into_pairs(t, c)
+
+        wa_codes = keep.tile([P, N], U32, name="wa_codes", tag="feature3", align_bytes=64)
+        wa_plane = held("wa_plane", [P, N], U8)
+        nc.vector.quantize_mx(out=wa_codes[:].bitcast(FP8X4), scales=wa_plane[:], in_=wa_bf[:])
+
+        page_plane = held("page_plane", [P, T2], U8)
+        out_2_words = out_2[0].rearrange("p m t -> p (m t)").bitcast(I32)
+        for c in range(CHUNKS):
+            round_into_pairs(PACK - 1, c)
+            grouped = held("grouped%d" % c, [P, BANK * PACK], BF16)
+            nc.vector.tensor_copy(
+                out=grouped[:].bitcast(I32).rearrange("p (m u) -> p m u", u=2),
+                in_=pairs[c][:].rearrange("p u m e -> p (u m e)").bitcast(I32).rearrange("p (u m) -> p m u", u=2),
+            )
+            page_codes = held("page_codes%d" % c, [P, BANK], U32)
+            nc.vector.quantize_mx(
+                out=page_codes[:].bitcast(FP8X4), scales=page_plane[:, chunks[c]], in_=grouped[:]
+            )
+            nc.sync.dma_start(out=out_2_words[:, chunks[c]], in_=page_codes[:].bitcast(I32))
+            if c == CHUNKS - 1:
+                for q in range(4):
+                    nc.sync.dma_start(
+                        out=out_3[0, 4 * q : 4 * q + 4, :].bitcast(I32),
+                        in_=page_plane[QUAD * q : QUAD * q + 4, :].bitcast(I32),
+                    )
+            for n in range(N // P):
+                rows = slice(n * P, (n + 1) * P)
+                a_bank, b_bank = bank(2 * n), bank(2 * n + 1)
+                nc.tensor.matmul_mx(
+                    out=a_bank[:],
+                    lhsT=wa_codes[:, rows].bitcast(FP8X4),
+                    lhsT_scale=wa_plane[:, rows],
+                    rhs=page_codes[:].bitcast(FP8X4),
+                    rhs_scale=page_plane[:, chunks[c]],
+                    start=True,
+                    stop=True,
+                )
+                nc.tensor.matmul_mx(
+                    out=b_bank[:],
+                    lhsT=wb_codes[:, 2 * n * P : 2 * (n + 1) * P].bitcast(FP4X4),
+                    lhsT_scale=wb_plane[:, rows],
+                    rhs=page_codes[:].bitcast(FP8X4),
+                    rhs_scale=page_plane[:, chunks[c]],
+                    start=True,
+                    stop=True,
+                )
+                y = ring.tile([P, BANK], F32, name="y")
+                nc.scalar.activation(out=y[:], in_=a_bank[:], func=ACT.Tanh)
+                nc.vector.tensor_tensor(y[:], b_bank[:], y[:], ALU.add)
+                nc.sync.dma_start(out=out_0[rows, chunks[c]], in_=y[:])

@@ -84,9 +84,8 @@ def tile_list_allergy_archive_kernel(
         page_rows = page0.rearrange("(p t) m -> t p m", t=PACK)
         page = [held("page%d" % t, [P, T2], F32) for t in range(PACK)]
         wgs_sb = held("wgs_sb", [P, PACK * S], F32)
-        early = shared.tile([P, PACK * S + PACK * N], F32, name="early", offset=0)
-        squares = early[:, : PACK * S]
-        wa_raw = early[:, PACK * S :]
+        squares = shared.tile([P, PACK * S], F32, name="squares", offset=0)
+        wa_raw = held("wa_raw", [P, PACK * N], F32)
 
         def load_wgs(lo, hi):
             for q in (0, 2, 1, 3):
@@ -95,24 +94,21 @@ def tile_list_allergy_archive_kernel(
         halves = [slice(h * BANK, (h + 1) * BANK) for h in range(HALVES)]
         load_wgs(0, BANK)
         nc.sync.dma_start(out=page[0][:], in_=page_rows[0])
-        load_wgs(BANK, 2 * S)
-        nc.sync.dma_start(out=page[1][:], in_=page_rows[1])
-        load_wgs(2 * S, 4 * S)
-        nc.sync.dma_start(out=wa_raw, in_=wa.rearrange("(p j) n -> p (j n)", j=PACK))
-        nc.sync.dma_start(out=page[2][:], in_=page_rows[2])
-        nc.sync.dma_start(out=page[3][:], in_=page_rows[3])
+        load_wgs(BANK, S)
+        for t in range(1, PACK):
+            load_wgs(t * S, (t + 1) * S)
+            nc.sync.dma_start(out=page[t][:], in_=page_rows[t])
+            if t == 1:
+                nc.sync.dma_start(out=wa_raw[:], in_=wa.rearrange("(p j) n -> p (j n)", j=PACK))
         wb_codes = held("wb_codes", [P, 2 * N], U8)
         nc.sync.dma_start(out=wb_codes[:].bitcast(I32), in_=wb_words[0].bitcast(I32))
-
-        picked_plane = held("picked_plane", [P, S], U8)
-        nc.vector.tensor_copy(picked_plane[:], tab_plane[:].indirect(pick[:]))
 
         w1_codes, w1_plane, picked = [], [], []
         for a in range(PASSES):
             w1_bf = held("w1_bf%d" % a, [P, PACK * H], BF16)
             nc.scalar.activation(
-                out=w1_bf[:].rearrange("p (t m j) -> p m j t", t=PACK, j=PACK),
-                in_=w1_raw[a][:].rearrange("p j (m t) -> p m j t", t=PACK),
+                out=w1_bf[:].rearrange("p (t m j) -> p t m j", t=PACK, j=PACK),
+                in_=w1_raw[a][:].rearrange("p j (m t) -> p t m j", t=PACK),
                 func=ACT.Copy,
             )
             w1_codes.append(held("w1_codes%d" % a, [P, H], U32))
@@ -123,6 +119,9 @@ def tile_list_allergy_archive_kernel(
                 nc.vector.tensor_copy(
                     picked[a][h][:], tab[a][:].indirect(pick[:, h * LIST_COLS : (h + 1) * LIST_COLS])
                 )
+            if a == 0:
+                picked_plane = keep.tile([P, S], U8, name="picked_plane", tag="tab0", align_bytes=64)
+                nc.vector.tensor_copy(picked_plane[:], tab_plane[:].indirect(pick[:]))
 
         q_bank = [[bank(HALVES * t + h) for h in range(HALVES)] for t in range(PACK)]
         for a in range(PASSES):
@@ -163,7 +162,7 @@ def tile_list_allergy_archive_kernel(
         wa_bf = held("wa_bf", [P, N * PACK], BF16)
         nc.scalar.activation(
             out=wa_bf[:].rearrange("p (c i j) -> p c j i", i=4, j=PACK),
-            in_=wa_raw.rearrange("p (j c i) -> p c j i", i=4, j=PACK),
+            in_=wa_raw[:].rearrange("p (j c i) -> p c j i", i=4, j=PACK),
             func=ACT.Copy,
         )
 

@@ -25,6 +25,7 @@ HALVES = S // BANK
 CHUNKS = T2 // BANK
 LIST_COLS = BANK // 16
 Y_BUFS = 10
+AHEAD = 2
 
 
 def tile_list_allergy_archive_kernel(
@@ -52,30 +53,28 @@ def tile_list_allergy_archive_kernel(
         wb_plane = held("wb_plane", [P, N], U8)
         nc.vector.memset(tab_plane[:].bitcast(I32), 0)
         nc.vector.memset(wb_plane[:].bitcast(I32), 0)
+
+        def load_w1(a):
+            rows = w1[a * P * PACK : (a + 1) * P * PACK, :]
+            nc.sync.dma_start(out=w1_raw[a][:], in_=rows.rearrange("(p j) c -> p j c", j=PACK))
+
+        def load_tab(a):
+            nc.sync.dma_start(
+                out=tab[a][:].bitcast(I32), in_=tab_words[a].rearrange("p n t -> p (n t)").bitcast(I32)
+            )
+
+        w1_raw = [held("w1_raw%d" % a, [P, PACK, H], F32) for a in range(PASSES)]
+        tab = [held("tab%d" % a, [P, T], U32) for a in range(PASSES)]
+        nc.sync.dma_start(pick[:], offs)
+        load_w1(0)
         for q in range(4):
-            nc.gpsimd.dma_start(
+            nc.sync.dma_start(
                 out=tab_plane[QUAD * q : QUAD * q + 4 * PASSES, :].bitcast(I32),
                 in_=tab_scales[:, 4 * q : 4 * q + 4, :].bitcast(I32),
             )
-        for q in range(4):
-            nc.gpsimd.dma_start(
-                out=wb_plane[QUAD * q : QUAD * q + 4, :].bitcast(I32),
-                in_=wb_scales[0, 4 * q : 4 * q + 4, :].bitcast(I32),
-            )
-
-        nc.sync.dma_start(pick[:], offs)
-        w1_raw, tab = [], []
-        for a in range(PASSES):
-            w1_raw.append(held("w1_raw%d" % a, [P, PACK, H], F32))
-            nc.sync.dma_start(
-                out=w1_raw[a][:],
-                in_=w1[a * P * PACK : (a + 1) * P * PACK, :].rearrange("(p j) c -> p j c", j=PACK),
-            )
-            tab.append(held("tab%d" % a, [P, T], U32))
-            nc.sync.dma_start(
-                out=tab[a][:].bitcast(I32),
-                in_=tab_words[a].rearrange("p n t -> p (n t)").bitcast(I32),
-            )
+        load_tab(0)
+        load_w1(1)
+        load_tab(1)
         nc.sync.dma_start(place[:], offs2)
         gain_sb = held("gain_sb", [P, PACK], F32)
         nc.sync.dma_start(out=gain_sb[:], in_=gain.rearrange("(p t) -> p t", t=PACK))
@@ -84,7 +83,6 @@ def tile_list_allergy_archive_kernel(
         page_rows = page0.rearrange("(p t) m -> t p m", t=PACK)
         page = [held("page%d" % t, [P, T2], F32) for t in range(PACK)]
         wgs_sb = held("wgs_sb", [P, PACK * S], F32)
-        squares = shared.tile([P, PACK * S], F32, name="squares", offset=0)
         wa_raw = held("wa_raw", [P, PACK * N], F32)
 
         def load_wgs(lo, hi):
@@ -102,15 +100,21 @@ def tile_list_allergy_archive_kernel(
                 nc.sync.dma_start(out=wa_raw[:], in_=wa.rearrange("(p j) n -> p (j n)", j=PACK))
         wb_codes = held("wb_codes", [P, 2 * N], U8)
         nc.sync.dma_start(out=wb_codes[:].bitcast(I32), in_=wb_words[0].bitcast(I32))
+        for q in range(4):
+            nc.sync.dma_start(
+                out=wb_plane[QUAD * q : QUAD * q + 4, :].bitcast(I32),
+                in_=wb_scales[0, 4 * q : 4 * q + 4, :].bitcast(I32),
+            )
 
+        picked_plane = held("picked_plane", [P, S], U8)
+        nc.vector.tensor_copy(picked_plane[:], tab_plane[:].indirect(pick[:]))
         w1_codes, w1_plane, picked = [], [], []
         for a in range(PASSES):
             w1_bf = held("w1_bf%d" % a, [P, PACK * H], BF16)
-            nc.scalar.activation(
-                out=w1_bf[:].rearrange("p (t m j) -> p t m j", t=PACK, j=PACK),
-                in_=w1_raw[a][:].rearrange("p j (m t) -> p t m j", t=PACK),
-                func=ACT.Copy,
-            )
+            dealt = w1_bf[:].rearrange("p (t m j) -> p t m j", t=PACK, j=PACK)
+            raw = w1_raw[a][:].rearrange("p j (m t) -> p t m j", t=PACK)
+            nc.scalar.activation(out=dealt[:, :2], in_=raw[:, :2], func=ACT.Copy)
+            nc.vector.tensor_copy(out=dealt[:, 2:], in_=raw[:, 2:])
             w1_codes.append(held("w1_codes%d" % a, [P, H], U32))
             w1_plane.append(held("w1_plane%d" % a, [P, H], U8))
             nc.vector.quantize_mx(out=w1_codes[a][:].bitcast(FP8X4), scales=w1_plane[a][:], in_=w1_bf[:])
@@ -119,9 +123,6 @@ def tile_list_allergy_archive_kernel(
                 nc.vector.tensor_copy(
                     picked[a][h][:], tab[a][:].indirect(pick[:, h * LIST_COLS : (h + 1) * LIST_COLS])
                 )
-            if a == 0:
-                picked_plane = keep.tile([P, S], U8, name="picked_plane", tag="tab0", align_bytes=64)
-                nc.vector.tensor_copy(picked_plane[:], tab_plane[:].indirect(pick[:]))
 
         q_bank = [[bank(HALVES * t + h) for h in range(HALVES)] for t in range(PACK)]
         for a in range(PASSES):
@@ -140,24 +141,15 @@ def tile_list_allergy_archive_kernel(
 
         feature = [held("feature%d" % t, [P, S], F32) for t in range(PACK)]
         pieces = [halves] + [[slice(0, S)]] * (PACK - 1)
-        wgs_gain = held("wgs_gain", [P, BANK], F32)
-        nc.scalar.activation(out=wgs_gain[:], in_=wgs_sb[:, :BANK], func=ACT.Copy, scale=gain_sb[:, 0:1])
-        factor = {}
         for t in range(PACK):
             for cols in pieces[t]:
-                wide = slice(t * S + cols.start, t * S + cols.stop)
+                squares = shared.tile([P, PACK * S], F32, name="squares", offset=0)
                 for h in range(cols.start // BANK, cols.stop // BANK):
-                    nc.scalar.activation(
-                        out=squares[:, t * S + h * BANK : t * S + (h + 1) * BANK], in_=q_bank[t][h][:], func=ACT.Square
-                    )
-                nc.scalar.activation(out=feature[t][:, cols], in_=squares[:, wide], func=ACT.Exp, scale=-1.0)
-                if wide.start == 0:
-                    factor[wide.start] = wgs_gain[:]
-                else:
-                    factor[wide.start] = wgs_sb[:, wide]
-                    nc.scalar.activation(
-                        out=feature[t][:, cols], in_=feature[t][:, cols], func=ACT.Copy, scale=gain_sb[:, t : t + 1]
-                    )
+                    nc.scalar.activation(out=squares[:, halves[h]], in_=q_bank[t][h][:], func=ACT.Square)
+                nc.scalar.activation(out=feature[t][:, cols], in_=squares[:, cols], func=ACT.Exp, scale=-1.0)
+                nc.scalar.activation(
+                    out=feature[t][:, cols], in_=feature[t][:, cols], func=ACT.Copy, scale=gain_sb[:, t : t + 1]
+                )
 
         wa_bf = held("wa_bf", [P, N * PACK], BF16)
         nc.scalar.activation(
@@ -181,7 +173,7 @@ def tile_list_allergy_archive_kernel(
                 nc.vector.tensor_tensor(
                     page[t][:].indirect(place[:, cols.start // 16 : cols.stop // 16]),
                     feature[t][:, cols],
-                    factor[t * S + cols.start],
+                    wgs_sb[:, t * S + cols.start : t * S + cols.stop],
                     ALU.mult,
                 )
             nc.sync.dma_start(out=out_1_rows[t], in_=page[t][:])
@@ -195,24 +187,21 @@ def tile_list_allergy_archive_kernel(
 
         page_plane = held("page_plane", [P, T2], U8)
         out_2_words = out_2[0].rearrange("p m t -> p (m t)").bitcast(I32)
-        for c in range(CHUNKS):
+        page_codes = [held("page_codes%d" % c, [P, BANK], U32) for c in range(CHUNKS)]
+
+        def quantise_chunk(c):
             round_into_pairs(PACK - 1, c)
             grouped = held("grouped%d" % c, [P, BANK * PACK], BF16)
             nc.vector.tensor_copy(
                 out=grouped[:].bitcast(I32).rearrange("p (m u) -> p m u", u=2),
                 in_=pairs[c][:].rearrange("p u m e -> p (u m e)").bitcast(I32).rearrange("p (u m) -> p m u", u=2),
             )
-            page_codes = held("page_codes%d" % c, [P, BANK], U32)
             nc.vector.quantize_mx(
-                out=page_codes[:].bitcast(FP8X4), scales=page_plane[:, chunks[c]], in_=grouped[:]
+                out=page_codes[c][:].bitcast(FP8X4), scales=page_plane[:, chunks[c]], in_=grouped[:]
             )
-            nc.sync.dma_start(out=out_2_words[:, chunks[c]], in_=page_codes[:].bitcast(I32))
-            if c == CHUNKS - 1:
-                for q in range(4):
-                    nc.sync.dma_start(
-                        out=out_3[0, 4 * q : 4 * q + 4, :].bitcast(I32),
-                        in_=page_plane[QUAD * q : QUAD * q + 4, :].bitcast(I32),
-                    )
+            nc.sync.dma_start(out=out_2_words[:, chunks[c]], in_=page_codes[c][:].bitcast(I32))
+
+        def multiply_chunk(c):
             for n in range(N // P):
                 rows = slice(n * P, (n + 1) * P)
                 a_bank, b_bank = bank(2 * n), bank(2 * n + 1)
@@ -220,7 +209,7 @@ def tile_list_allergy_archive_kernel(
                     out=a_bank[:],
                     lhsT=wa_codes[:, rows].bitcast(FP8X4),
                     lhsT_scale=wa_plane[:, rows],
-                    rhs=page_codes[:].bitcast(FP8X4),
+                    rhs=page_codes[c][:].bitcast(FP8X4),
                     rhs_scale=page_plane[:, chunks[c]],
                     start=True,
                     stop=True,
@@ -229,7 +218,7 @@ def tile_list_allergy_archive_kernel(
                     out=b_bank[:],
                     lhsT=wb_codes[:, 2 * n * P : 2 * (n + 1) * P].bitcast(FP4X4),
                     lhsT_scale=wb_plane[:, rows],
-                    rhs=page_codes[:].bitcast(FP8X4),
+                    rhs=page_codes[c][:].bitcast(FP8X4),
                     rhs_scale=page_plane[:, chunks[c]],
                     start=True,
                     stop=True,
@@ -238,3 +227,16 @@ def tile_list_allergy_archive_kernel(
                 nc.scalar.activation(out=y[:], in_=a_bank[:], func=ACT.Tanh)
                 nc.vector.tensor_tensor(y[:], b_bank[:], y[:], ALU.add)
                 nc.sync.dma_start(out=out_0[rows, chunks[c]], in_=y[:])
+
+        for c in range(AHEAD):
+            quantise_chunk(c)
+        for c in range(CHUNKS):
+            if c + AHEAD < CHUNKS:
+                quantise_chunk(c + AHEAD)
+            if c + AHEAD == CHUNKS - 1:
+                for q in range(4):
+                    nc.sync.dma_start(
+                        out=out_3[0, 4 * q : 4 * q + 4, :].bitcast(I32),
+                        in_=page_plane[QUAD * q : QUAD * q + 4, :].bitcast(I32),
+                    )
+            multiply_chunk(c)

@@ -1,6 +1,7 @@
 from contextlib import ExitStack
 
 import concourse.mybir as mybir
+from concourse.masks import make_identity
 
 K, T, S, T2, H, N = 1024, 4096, 1024, 2048, 512, 512
 FLOPS = 2 * K * H * S + 2 * 2 * H * N * T2
@@ -19,13 +20,19 @@ ALU = mybir.AluOpType
 P = 128
 PACK = 4
 QUAD = 32
+QUADS = P // QUAD
+SCALE_ROWS = 4
 BANK = 512
+GROUP = 16
 PASSES = K // (P * PACK)
 HALVES = S // BANK
-CHUNKS = T2 // BANK
-LIST_COLS = BANK // 16
-Y_BUFS = 10
+WIDTHS = (BANK // 2, BANK // 2, BANK, BANK, BANK)
+CHUNKS = len(WIDTHS)
+BLOCKS = BANK // P
+EARLY_SLICES = 2
+RUN = 4
 AHEAD = 2
+Y_BUFS = 10
 
 
 def tile_list_allergy_archive_kernel(
@@ -37,17 +44,21 @@ def tile_list_allergy_archive_kernel(
         lists = ctx.enter_context(tc.tile_pool(name="lists", bufs=1))
         keep = ctx.enter_context(tc.tile_pool(name="keep", bufs=1))
         shared = ctx.enter_context(tc.tile_pool(name="shared", bufs=1))
+        reused = ctx.enter_context(tc.tile_pool(name="reused", bufs=1))
         ring = ctx.enter_context(tc.tile_pool(name="ring", bufs=Y_BUFS))
         psum = ctx.enter_context(tc.psum_pool(name="psum", bufs=1))
 
-        def held(name, shape, dtype):
-            return keep.tile(shape, dtype, name=name, tag=name, align_bytes=64)
+        def held(name, shape, dtype, after=None):
+            return keep.tile(shape, dtype, name=name, tag=after or name, align_bytes=64)
 
         def bank(i):
             return psum.tile([P, BANK], F32, name="bank%d" % i)
 
-        pick = lists.tile([P, S // 16], U16, name="pick")
-        place = lists.tile([P, S // 16], U16, name="place")
+        halves = [slice(h * BANK, (h + 1) * BANK) for h in range(HALVES)]
+        chunks = [slice(sum(WIDTHS[:c]), sum(WIDTHS[: c + 1])) for c in range(CHUNKS)]
+
+        pick = lists.tile([P, S // GROUP], U16, name="pick")
+        place = lists.tile([P, S // GROUP], U16, name="place")
 
         tab_plane = held("tab_plane", [P, T], U8)
         wb_plane = held("wb_plane", [P, N], U8)
@@ -63,66 +74,96 @@ def tile_list_allergy_archive_kernel(
                 out=tab[a][:].bitcast(I32), in_=tab_words[a].rearrange("p n t -> p (n t)").bitcast(I32)
             )
 
-        w1_raw = [held("w1_raw%d" % a, [P, PACK, H], F32) for a in range(PASSES)]
+        w1_raw = [held("w1_raw0", [P, PACK, H], F32), reused.tile([P, PACK, H], F32, name="w1_raw1", offset=0)]
         tab = [held("tab%d" % a, [P, T], U32) for a in range(PASSES)]
+        wgs_sb = held("wgs_sb", [P, S], F32)
+        gain_sb = held("gain_sb", [P, PACK], F32)
         nc.sync.dma_start(pick[:], offs)
-        load_w1(0)
-        for q in range(4):
+        nc.sync.dma_start(out=wgs_sb[:], in_=wgs)
+        for q in range(QUADS):
             nc.sync.dma_start(
-                out=tab_plane[QUAD * q : QUAD * q + 4 * PASSES, :].bitcast(I32),
-                in_=tab_scales[:, 4 * q : 4 * q + 4, :].bitcast(I32),
+                out=tab_plane[QUAD * q : QUAD * q + SCALE_ROWS * PASSES, :].bitcast(I32),
+                in_=tab_scales[:, SCALE_ROWS * q : SCALE_ROWS * (q + 1), :].bitcast(I32),
             )
+        load_w1(0)
+        nc.sync.dma_start(out=gain_sb[:], in_=gain.rearrange("(p t) -> p t", t=PACK))
         load_tab(0)
         load_w1(1)
         load_tab(1)
         nc.sync.dma_start(place[:], offs2)
-        gain_sb = held("gain_sb", [P, PACK], F32)
-        nc.sync.dma_start(out=gain_sb[:], in_=gain.rearrange("(p t) -> p t", t=PACK))
 
-        wgs_rows = wgs.rearrange("(p t) j -> p (t j)", t=PACK)
         page_rows = page0.rearrange("(p t) m -> t p m", t=PACK)
         page = [held("page%d" % t, [P, T2], F32) for t in range(PACK)]
-        wgs_sb = held("wgs_sb", [P, PACK * S], F32)
         wa_raw = held("wa_raw", [P, PACK * N], F32)
-
-        def load_wgs(lo, hi):
-            for q in (0, 2, 1, 3):
-                nc.sync.dma_start(out=wgs_sb[QUAD * q : QUAD * (q + 1), lo:hi], in_=wgs_rows[:, lo:hi])
-
-        halves = [slice(h * BANK, (h + 1) * BANK) for h in range(HALVES)]
-        load_wgs(0, BANK)
         nc.sync.dma_start(out=page[0][:], in_=page_rows[0])
-        load_wgs(BANK, S)
-        for t in range(1, PACK):
-            load_wgs(t * S, (t + 1) * S)
-            nc.sync.dma_start(out=page[t][:], in_=page_rows[t])
-            if t == 1:
-                nc.sync.dma_start(out=wa_raw[:], in_=wa.rearrange("(p j) n -> p (j n)", j=PACK))
+        nc.sync.dma_start(out=page[1][:], in_=page_rows[1])
+        nc.sync.dma_start(out=wa_raw[:], in_=wa.rearrange("(p j) n -> p (j n)", j=PACK))
+        nc.sync.dma_start(out=page[2][:], in_=page_rows[2])
+        nc.sync.dma_start(out=page[3][:], in_=page_rows[3])
         wb_codes = held("wb_codes", [P, 2 * N], U8)
         nc.sync.dma_start(out=wb_codes[:].bitcast(I32), in_=wb_words[0].bitcast(I32))
-        for q in range(4):
+        for q in range(QUADS):
             nc.sync.dma_start(
-                out=wb_plane[QUAD * q : QUAD * q + 4, :].bitcast(I32),
-                in_=wb_scales[0, 4 * q : 4 * q + 4, :].bitcast(I32),
+                out=wb_plane[QUAD * q : QUAD * q + SCALE_ROWS, :].bitcast(I32),
+                in_=wb_scales[0, SCALE_ROWS * q : SCALE_ROWS * (q + 1), :].bitcast(I32),
             )
 
-        picked_plane = held("picked_plane", [P, S], U8)
-        nc.vector.tensor_copy(picked_plane[:], tab_plane[:].indirect(pick[:]))
+        identity = held("identity", [P, P], F32)
+        make_identity(nc, identity[:])
+        spread = shared.tile([P, HALVES, BLOCKS, PACK, P], F32, name="spread", offset=0)
+        for h, copy_out in enumerate((nc.scalar.copy, nc.vector.tensor_copy)):
+            turned = bank(HALVES * (PACK - 1) + h)
+            for g in range(BLOCKS):
+                j0 = h * BANK + g * P
+                nc.tensor.transpose(turned[:, g * P : (g + 1) * P], wgs_sb[:, j0 : j0 + P], identity[:])
+            by_slice = turned[:].rearrange("p (g i t) -> p g t i", g=BLOCKS, t=PACK)
+            copy_out(
+                out=spread[:, h].rearrange("p g t (q i) -> p g t q i", i=QUAD),
+                in_=by_slice.unsqueeze(3).to_broadcast([P, BLOCKS, PACK, QUADS, QUAD]),
+            )
+
+        weight = []
+
+        def deal_weight(t, tile):
+            weight.append(tile)
+            for h in range(HALVES):
+                back = bank(HALVES * t + h)
+                for g in range(BLOCKS):
+                    nc.tensor.transpose(back[:, g * P : (g + 1) * P], spread[:, h, g, t, :], identity[:])
+                nc.scalar.activation(
+                    out=tile[:, halves[h]], in_=back[:], func=ACT.Copy, scale=gain_sb[:, t : t + 1]
+                )
+
         w1_codes, w1_plane, picked = [], [], []
-        for a in range(PASSES):
+
+        def quantise_w1(a):
             w1_bf = held("w1_bf%d" % a, [P, PACK * H], BF16)
             dealt = w1_bf[:].rearrange("p (t m j) -> p t m j", t=PACK, j=PACK)
             raw = w1_raw[a][:].rearrange("p j (m t) -> p t m j", t=PACK)
-            nc.scalar.activation(out=dealt[:, :2], in_=raw[:, :2], func=ACT.Copy)
-            nc.vector.tensor_copy(out=dealt[:, 2:], in_=raw[:, 2:])
+            nc.scalar.activation(out=dealt[:, : PACK // 2], in_=raw[:, : PACK // 2], func=ACT.Copy)
+            nc.vector.tensor_copy(out=dealt[:, PACK // 2 :], in_=raw[:, PACK // 2 :])
             w1_codes.append(held("w1_codes%d" % a, [P, H], U32))
             w1_plane.append(held("w1_plane%d" % a, [P, H], U8))
             nc.vector.quantize_mx(out=w1_codes[a][:].bitcast(FP8X4), scales=w1_plane[a][:], in_=w1_bf[:])
+
+        def entries(offsets, cols):
+            return offsets[:, cols.start // GROUP : cols.stop // GROUP]
+
+        def gather_words(a):
             picked.append([held("picked%d_%d" % (a, h), [P, BANK], U32) for h in range(HALVES)])
             for h in range(HALVES):
-                nc.vector.tensor_copy(
-                    picked[a][h][:], tab[a][:].indirect(pick[:, h * LIST_COLS : (h + 1) * LIST_COLS])
-                )
+                nc.vector.tensor_copy(picked[a][h][:], tab[a][:].indirect(entries(pick, halves[h])))
+
+        quantise_w1(0)
+        for t in range(EARLY_SLICES):
+            deal_weight(t, held("weight%d" % t, [P, S], F32))
+        picked_plane = held("picked_plane", [P, S], U8)
+        nc.vector.tensor_copy(picked_plane[:], tab_plane[:].indirect(pick[:]))
+        gather_words(0)
+        quantise_w1(1)
+        for t in range(EARLY_SLICES, PACK):
+            deal_weight(t, reused.tile([P, S], F32, name="weight%d" % t, offset=(t - EARLY_SLICES) * S * 4))
+        gather_words(1)
 
         q_bank = [[bank(HALVES * t + h) for h in range(HALVES)] for t in range(PACK)]
         for a in range(PASSES):
@@ -134,7 +175,7 @@ def tile_list_allergy_archive_kernel(
                         lhsT=w1_codes[a][:, rows].bitcast(FP8X4),
                         lhsT_scale=w1_plane[a][:, rows],
                         rhs=picked[a][h][:].bitcast(FP8X4),
-                        rhs_scale=picked_plane[4 * a :, halves[h]],
+                        rhs_scale=picked_plane[SCALE_ROWS * a :, halves[h]],
                         start=(a == 0),
                         stop=(a == PASSES - 1),
                     )
@@ -147,21 +188,18 @@ def tile_list_allergy_archive_kernel(
                 for h in range(cols.start // BANK, cols.stop // BANK):
                     nc.scalar.activation(out=squares[:, halves[h]], in_=q_bank[t][h][:], func=ACT.Square)
                 nc.scalar.activation(out=feature[t][:, cols], in_=squares[:, cols], func=ACT.Exp, scale=-1.0)
-                nc.scalar.activation(
-                    out=feature[t][:, cols], in_=feature[t][:, cols], func=ACT.Copy, scale=gain_sb[:, t : t + 1]
-                )
 
         wa_bf = held("wa_bf", [P, N * PACK], BF16)
         nc.scalar.activation(
-            out=wa_bf[:].rearrange("p (c i j) -> p c j i", i=4, j=PACK),
-            in_=wa_raw[:].rearrange("p (j c i) -> p c j i", i=4, j=PACK),
+            out=wa_bf[:].rearrange("p (c i j) -> p c j i", i=RUN, j=PACK),
+            in_=wa_raw[:].rearrange("p (j c i) -> p c j i", i=RUN, j=PACK),
             func=ACT.Copy,
         )
 
         out_1_rows = out_1.rearrange("(p t) m -> t p m", t=PACK)
-        chunks = [slice(c * BANK, (c + 1) * BANK) for c in range(CHUNKS)]
+        column_bytes = PACK * 2
         pairs = [
-            shared.tile([P, 2, BANK, 2], BF16, name="pairs%d" % c, offset=c * BANK * PACK * 2)
+            shared.tile([P, 2, WIDTHS[c], 2], BF16, name="pairs%d" % c, offset=chunks[c].start * column_bytes)
             for c in range(CHUNKS)
         ]
 
@@ -171,27 +209,24 @@ def tile_list_allergy_archive_kernel(
         for t in range(PACK):
             for cols in pieces[t]:
                 nc.vector.tensor_tensor(
-                    page[t][:].indirect(place[:, cols.start // 16 : cols.stop // 16]),
-                    feature[t][:, cols],
-                    wgs_sb[:, t * S + cols.start : t * S + cols.stop],
-                    ALU.mult,
+                    page[t][:].indirect(entries(place, cols)), feature[t][:, cols], weight[t][:, cols], ALU.mult
                 )
             nc.sync.dma_start(out=out_1_rows[t], in_=page[t][:])
             if t < PACK - 1:
                 for c in range(CHUNKS):
                     round_into_pairs(t, c)
 
-        wa_codes = keep.tile([P, N], U32, name="wa_codes", tag="feature3", align_bytes=64)
+        wa_codes = held("wa_codes", [P, N], U32, after="feature%d" % (PACK - 1))
         wa_plane = held("wa_plane", [P, N], U8)
         nc.vector.quantize_mx(out=wa_codes[:].bitcast(FP8X4), scales=wa_plane[:], in_=wa_bf[:])
 
         page_plane = held("page_plane", [P, T2], U8)
         out_2_words = out_2[0].rearrange("p m t -> p (m t)").bitcast(I32)
-        page_codes = [held("page_codes%d" % c, [P, BANK], U32) for c in range(CHUNKS)]
+        page_codes = [held("page_codes%d" % c, [P, WIDTHS[c]], U32) for c in range(CHUNKS)]
 
         def quantise_chunk(c):
             round_into_pairs(PACK - 1, c)
-            grouped = held("grouped%d" % c, [P, BANK * PACK], BF16)
+            grouped = held("grouped%d" % c, [P, WIDTHS[c] * PACK], BF16)
             nc.vector.tensor_copy(
                 out=grouped[:].bitcast(I32).rearrange("p (m u) -> p m u", u=2),
                 in_=pairs[c][:].rearrange("p u m e -> p (u m e)").bitcast(I32).rearrange("p (u m) -> p m u", u=2),
@@ -201,12 +236,19 @@ def tile_list_allergy_archive_kernel(
             )
             nc.sync.dma_start(out=out_2_words[:, chunks[c]], in_=page_codes[c][:].bitcast(I32))
 
+        def store_page_plane():
+            for q in range(QUADS):
+                nc.sync.dma_start(
+                    out=out_3[0, SCALE_ROWS * q : SCALE_ROWS * (q + 1), :].bitcast(I32),
+                    in_=page_plane[QUAD * q : QUAD * q + SCALE_ROWS, :].bitcast(I32),
+                )
+
         def multiply_chunk(c):
             for n in range(N // P):
                 rows = slice(n * P, (n + 1) * P)
-                a_bank, b_bank = bank(2 * n), bank(2 * n + 1)
+                a_sum, b_sum = bank(2 * n)[:, : WIDTHS[c]], bank(2 * n + 1)[:, : WIDTHS[c]]
                 nc.tensor.matmul_mx(
-                    out=a_bank[:],
+                    out=a_sum,
                     lhsT=wa_codes[:, rows].bitcast(FP8X4),
                     lhsT_scale=wa_plane[:, rows],
                     rhs=page_codes[c][:].bitcast(FP8X4),
@@ -215,17 +257,17 @@ def tile_list_allergy_archive_kernel(
                     stop=True,
                 )
                 nc.tensor.matmul_mx(
-                    out=b_bank[:],
-                    lhsT=wb_codes[:, 2 * n * P : 2 * (n + 1) * P].bitcast(FP4X4),
+                    out=b_sum,
+                    lhsT=wb_codes[:, 2 * rows.start : 2 * rows.stop].bitcast(FP4X4),
                     lhsT_scale=wb_plane[:, rows],
                     rhs=page_codes[c][:].bitcast(FP8X4),
                     rhs_scale=page_plane[:, chunks[c]],
                     start=True,
                     stop=True,
                 )
-                y = ring.tile([P, BANK], F32, name="y")
-                nc.scalar.activation(out=y[:], in_=a_bank[:], func=ACT.Tanh)
-                nc.vector.tensor_tensor(y[:], b_bank[:], y[:], ALU.add)
+                y = ring.tile([P, WIDTHS[c]], F32, name="y")
+                nc.scalar.activation(out=y[:], in_=a_sum, func=ACT.Tanh)
+                nc.vector.tensor_tensor(y[:], b_sum, y[:], ALU.add)
                 nc.sync.dma_start(out=out_0[rows, chunks[c]], in_=y[:])
 
         for c in range(AHEAD):
@@ -234,9 +276,5 @@ def tile_list_allergy_archive_kernel(
             if c + AHEAD < CHUNKS:
                 quantise_chunk(c + AHEAD)
             if c + AHEAD == CHUNKS - 1:
-                for q in range(4):
-                    nc.sync.dma_start(
-                        out=out_3[0, 4 * q : 4 * q + 4, :].bitcast(I32),
-                        in_=page_plane[QUAD * q : QUAD * q + 4, :].bitcast(I32),
-                    )
+                store_page_plane()
             multiply_chunk(c)

@@ -26,12 +26,14 @@ BANK = 512
 GROUP = 16
 PASSES = K // (P * PACK)
 HALVES = S // BANK
-WIDTHS = (BANK // 2, BANK // 2, BANK, BANK, BANK)
+WIDTHS = (BANK // 2, BANK, BANK, BANK, BANK // 2)
 CHUNKS = len(WIDTHS)
 BLOCKS = BANK // P
 EARLY_SLICES = 2
 RUN = 4
 AHEAD = 2
+BANKS = 8
+FIRST = 256
 Y_BUFS = 10
 
 
@@ -165,31 +167,53 @@ def tile_list_allergy_archive_kernel(
             deal_weight(t, reused.tile([P, S], F32, name="weight%d" % t, offset=(t - EARLY_SLICES) * S * 4))
         gather_words(1)
 
-        q_bank = [[bank(HALVES * t + h) for h in range(HALVES)] for t in range(PACK)]
-        for a in range(PASSES):
-            for h in range(HALVES):
-                for t in range(PACK):
-                    rows = slice(t * P, (t + 1) * P)
-                    nc.tensor.matmul_mx(
-                        out=q_bank[t][h][:],
-                        lhsT=w1_codes[a][:, rows].bitcast(FP8X4),
-                        lhsT_scale=w1_plane[a][:, rows],
-                        rhs=picked[a][h][:].bitcast(FP8X4),
-                        rhs_scale=picked_plane[SCALE_ROWS * a :, halves[h]],
-                        start=(a == 0),
-                        stop=(a == PASSES - 1),
-                    )
+        pieces = [(0, slice(0, FIRST)), (0, slice(FIRST, S))]
+        pieces.extend((t, slice(0, S)) for t in range(1, PACK))
+
+        def bank_runs(cols):
+            if cols.stop == FIRST:
+                return [slice(0, FIRST // 2), slice(FIRST // 2, FIRST)]
+            return [
+                slice(max(cols.start, half.start), min(cols.stop, half.stop))
+                for half in halves
+                if cols.start < half.stop and half.start < cols.stop
+            ]
+
+        runs = [(t, run) for t, cols in pieces for run in bank_runs(cols)]
+        q_sum = {}
+
+        def first_stage_pass(a, t, run):
+            rows = slice(t * P, (t + 1) * P)
+            h = run.start // BANK
+            nc.tensor.matmul_mx(
+                out=q_sum[t, run.start],
+                lhsT=w1_codes[a][:, rows].bitcast(FP8X4),
+                lhsT_scale=w1_plane[a][:, rows],
+                rhs=picked[a][h][:, run.start - h * BANK : run.stop - h * BANK].bitcast(FP8X4),
+                rhs_scale=picked_plane[SCALE_ROWS * a :, run],
+                start=(a == 0),
+                stop=(a == PASSES - 1),
+            )
+
+        for i, (t, run) in enumerate(runs[:BANKS]):
+            q_sum[t, run.start] = bank(i)[:, : run.stop - run.start]
+            first_stage_pass(0, t, run)
 
         feature = [held("feature%d" % t, [P, S], F32) for t in range(PACK)]
-        pieces = [halves] + [[slice(0, S)]] * (PACK - 1)
-        for t in range(PACK):
-            for cols in pieces[t]:
-                squares = shared.tile([P, PACK * S], F32, name="squares", offset=0)
-                for h in range(cols.start // BANK, cols.stop // BANK):
-                    nc.scalar.activation(out=squares[:, halves[h]], in_=q_bank[t][h][:], func=ACT.Square)
-                nc.scalar.activation(out=feature[t][:, cols], in_=squares[:, cols], func=ACT.Exp, scale=-1.0)
+        for t, cols in pieces:
+            if cols.start == 0:
+                squares = shared.tile([P, PACK * S + N * PACK // 2], F32, name="squares", offset=0)
+            for run in bank_runs(cols):
+                i = runs.index((t, run))
+                if i >= BANKS:
+                    q_sum[t, run.start] = bank(i % BANKS)[:, : run.stop - run.start]
+                    first_stage_pass(0, t, run)
+                first_stage_pass(1, t, run)
+                nc.scalar.activation(out=squares[:, run], in_=q_sum[t, run.start], func=ACT.Square)
+            for run in bank_runs(cols) if cols.stop == FIRST else [cols]:
+                nc.scalar.activation(out=feature[t][:, run], in_=squares[:, run], func=ACT.Exp, scale=-1.0)
 
-        wa_bf = held("wa_bf", [P, N * PACK], BF16)
+        wa_bf = shared.tile([P, N * PACK], BF16, name="wa_bf", offset=PACK * S * 4, align_bytes=64)
         nc.scalar.activation(
             out=wa_bf[:].rearrange("p (c i j) -> p c j i", i=RUN, j=PACK),
             in_=wa_raw[:].rearrange("p (j c i) -> p c j i", i=RUN, j=PACK),
@@ -206,15 +230,15 @@ def tile_list_allergy_archive_kernel(
         def round_into_pairs(t, c):
             nc.scalar.activation(out=pairs[c][:, t // 2, :, t % 2], in_=page[t][:, chunks[c]], func=ACT.Copy)
 
-        for t in range(PACK):
-            for cols in pieces[t]:
-                nc.vector.tensor_tensor(
-                    page[t][:].indirect(entries(place, cols)), feature[t][:, cols], weight[t][:, cols], ALU.mult
-                )
-            nc.sync.dma_start(out=out_1_rows[t], in_=page[t][:])
-            if t < PACK - 1:
-                for c in range(CHUNKS):
-                    round_into_pairs(t, c)
+        for t, cols in pieces:
+            nc.vector.tensor_tensor(
+                page[t][:].indirect(entries(place, cols)), feature[t][:, cols], weight[t][:, cols], ALU.mult
+            )
+            if cols.stop == S:
+                nc.sync.dma_start(out=out_1_rows[t], in_=page[t][:])
+                if t < PACK - 1:
+                    for c in range(CHUNKS):
+                        round_into_pairs(t, c)
 
         wa_codes = held("wa_codes", [P, N], U32, after="feature%d" % (PACK - 1))
         wa_plane = held("wa_plane", [P, N], U8)
@@ -226,8 +250,9 @@ def tile_list_allergy_archive_kernel(
 
         def quantise_chunk(c):
             round_into_pairs(PACK - 1, c)
-            grouped = held("grouped%d" % c, [P, WIDTHS[c] * PACK], BF16)
-            nc.vector.tensor_copy(
+            wide = c >= AHEAD
+            grouped = held("grouped_wide" if wide else "grouped%d" % c, [P, WIDTHS[c] * PACK], BF16)
+            (nc.gpsimd if wide else nc.vector).tensor_copy(
                 out=grouped[:].bitcast(I32).rearrange("p (m u) -> p m u", u=2),
                 in_=pairs[c][:].rearrange("p u m e -> p (u m e)").bitcast(I32).rearrange("p (u m) -> p m u", u=2),
             )

@@ -26,7 +26,7 @@ BANK = 512
 GROUP = 16
 PASSES = K // (P * PACK)
 HALVES = S // BANK
-WIDTHS = (BANK // 2, BANK, BANK, BANK, BANK // 2)
+WIDTHS = (BANK // 2, BANK // 2, BANK, BANK, BANK)
 CHUNKS = len(WIDTHS)
 BLOCKS = BANK // P
 EARLY_SLICES = 2
@@ -34,7 +34,8 @@ RUN = 4
 AHEAD = 2
 BANKS = 8
 FIRST = 256
-Y_BUFS = 10
+WARM = 3
+Y_BUFS = 8
 
 
 def tile_list_allergy_archive_kernel(
@@ -80,8 +81,8 @@ def tile_list_allergy_archive_kernel(
         tab = [held("tab%d" % a, [P, T], U32) for a in range(PASSES)]
         wgs_sb = held("wgs_sb", [P, S], F32)
         gain_sb = held("gain_sb", [P, PACK], F32)
-        nc.sync.dma_start(pick[:], offs)
         nc.sync.dma_start(out=wgs_sb[:], in_=wgs)
+        nc.sync.dma_start(pick[:], offs)
         for q in range(QUADS):
             nc.sync.dma_start(
                 out=tab_plane[QUAD * q : QUAD * q + SCALE_ROWS * PASSES, :].bitcast(I32),
@@ -91,8 +92,8 @@ def tile_list_allergy_archive_kernel(
         nc.sync.dma_start(out=gain_sb[:], in_=gain.rearrange("(p t) -> p t", t=PACK))
         load_tab(0)
         load_w1(1)
-        load_tab(1)
         nc.sync.dma_start(place[:], offs2)
+        load_tab(1)
 
         page_rows = page0.rearrange("(p t) m -> t p m", t=PACK)
         page = [held("page%d" % t, [P, T2], F32) for t in range(PACK)]
@@ -167,8 +168,8 @@ def tile_list_allergy_archive_kernel(
             deal_weight(t, reused.tile([P, S], F32, name="weight%d" % t, offset=(t - EARLY_SLICES) * S * 4))
         gather_words(1)
 
-        pieces = [(0, slice(0, FIRST)), (0, slice(FIRST, S))]
-        pieces.extend((t, slice(0, S)) for t in range(1, PACK))
+        pieces = [(0, slice(0, FIRST)), (1, halves[0]), (0, slice(FIRST, S)), (1, halves[1])]
+        pieces.extend((t, slice(0, S)) for t in range(2, PACK))
 
         def bank_runs(cols):
             if cols.stop == FIRST:
@@ -201,7 +202,7 @@ def tile_list_allergy_archive_kernel(
 
         feature = [held("feature%d" % t, [P, S], F32) for t in range(PACK)]
         for t, cols in pieces:
-            if cols.start == 0:
+            if True:
                 squares = shared.tile([P, PACK * S + N * PACK // 2], F32, name="squares", offset=0)
             for run in bank_runs(cols):
                 i = runs.index((t, run))
@@ -244,62 +245,92 @@ def tile_list_allergy_archive_kernel(
         wa_plane = held("wa_plane", [P, N], U8)
         nc.vector.quantize_mx(out=wa_codes[:].bitcast(FP8X4), scales=wa_plane[:], in_=wa_bf[:])
 
+        for i in range(WARM):
+            nc.tensor.matmul_mx(
+                out=bank(BANKS - 1 - i)[:],
+                lhsT=wa_codes[:, :P].bitcast(FP8X4),
+                lhsT_scale=wa_plane[:, :P],
+                rhs=wa_codes[:].bitcast(FP8X4),
+                rhs_scale=wa_plane[:],
+                start=True,
+                stop=True,
+            )
+
         page_plane = held("page_plane", [P, T2], U8)
         out_2_words = out_2[0].rearrange("p m t -> p (m t)").bitcast(I32)
-        page_codes = [held("page_codes%d" % c, [P, WIDTHS[c]], U32) for c in range(CHUNKS)]
+        page_codes = held("page_codes", [P, T2], U32)
 
         def quantise_chunk(c):
             round_into_pairs(PACK - 1, c)
-            wide = c >= AHEAD
+            wide = WIDTHS[c] == BANK
             grouped = held("grouped_wide" if wide else "grouped%d" % c, [P, WIDTHS[c] * PACK], BF16)
-            (nc.gpsimd if wide else nc.vector).tensor_copy(
+            (nc.gpsimd if c > 2 else nc.vector).tensor_copy(
                 out=grouped[:].bitcast(I32).rearrange("p (m u) -> p m u", u=2),
                 in_=pairs[c][:].rearrange("p u m e -> p (u m e)").bitcast(I32).rearrange("p (u m) -> p m u", u=2),
             )
             nc.vector.quantize_mx(
-                out=page_codes[c][:].bitcast(FP8X4), scales=page_plane[:, chunks[c]], in_=grouped[:]
+                out=page_codes[:, chunks[c]].bitcast(FP8X4), scales=page_plane[:, chunks[c]], in_=grouped[:]
             )
-            nc.sync.dma_start(out=out_2_words[:, chunks[c]], in_=page_codes[c][:].bitcast(I32))
 
-        def store_page_plane():
+        def store_codes(cols):
+            nc.sync.dma_start(out=out_2_words[:, cols], in_=page_codes[:, cols].bitcast(I32))
+
+        def store_page_plane(cols):
             for q in range(QUADS):
                 nc.sync.dma_start(
-                    out=out_3[0, SCALE_ROWS * q : SCALE_ROWS * (q + 1), :].bitcast(I32),
-                    in_=page_plane[QUAD * q : QUAD * q + SCALE_ROWS, :].bitcast(I32),
+                    out=out_3[0, SCALE_ROWS * q : SCALE_ROWS * (q + 1), cols].bitcast(I32),
+                    in_=page_plane[QUAD * q : QUAD * q + SCALE_ROWS, cols].bitcast(I32),
                 )
 
-        def multiply_chunk(c):
-            for n in range(N // P):
-                rows = slice(n * P, (n + 1) * P)
-                a_sum, b_sum = bank(2 * n)[:, : WIDTHS[c]], bank(2 * n + 1)[:, : WIDTHS[c]]
-                nc.tensor.matmul_mx(
-                    out=a_sum,
-                    lhsT=wa_codes[:, rows].bitcast(FP8X4),
-                    lhsT_scale=wa_plane[:, rows],
-                    rhs=page_codes[c][:].bitcast(FP8X4),
-                    rhs_scale=page_plane[:, chunks[c]],
-                    start=True,
-                    stop=True,
-                )
-                nc.tensor.matmul_mx(
-                    out=b_sum,
-                    lhsT=wb_codes[:, 2 * rows.start : 2 * rows.stop].bitcast(FP4X4),
-                    lhsT_scale=wb_plane[:, rows],
-                    rhs=page_codes[c][:].bitcast(FP8X4),
-                    rhs_scale=page_plane[:, chunks[c]],
-                    start=True,
-                    stop=True,
-                )
-                y = ring.tile([P, WIDTHS[c]], F32, name="y")
-                nc.scalar.activation(out=y[:], in_=a_sum, func=ACT.Tanh)
-                nc.vector.tensor_tensor(y[:], b_sum, y[:], ALU.add)
-                nc.sync.dma_start(out=out_0[rows, chunks[c]], in_=y[:])
+        done = []
 
-        for c in range(AHEAD):
-            quantise_chunk(c)
-        for c in range(CHUNKS):
-            if c + AHEAD < CHUNKS:
-                quantise_chunk(c + AHEAD)
-            if c + AHEAD == CHUNKS - 1:
-                store_page_plane()
-            multiply_chunk(c)
+        def multiply(n, cols, y):
+            rows = slice(n * P, (n + 1) * P)
+            first = 2 * len(done) % BANKS
+            done.append((n, cols))
+            a_sum, b_sum = bank(first), bank(first + 1)
+            nc.tensor.matmul_mx(
+                out=a_sum[:],
+                lhsT=wa_codes[:, rows].bitcast(FP8X4),
+                lhsT_scale=wa_plane[:, rows],
+                rhs=page_codes[:, cols].bitcast(FP8X4),
+                rhs_scale=page_plane[:, cols],
+                start=True,
+                stop=True,
+            )
+            nc.tensor.matmul_mx(
+                out=b_sum[:],
+                lhsT=wb_codes[:, 2 * rows.start : 2 * rows.stop].bitcast(FP4X4),
+                lhsT_scale=wb_plane[:, rows],
+                rhs=page_codes[:, cols].bitcast(FP8X4),
+                rhs_scale=page_plane[:, cols],
+                start=True,
+                stop=True,
+            )
+            nc.scalar.activation(out=y, in_=a_sum[:], func=ACT.Tanh)
+            nc.vector.tensor_tensor(y, b_sum[:], y, ALU.add)
+
+        def multiply_and_store(n, cols):
+            y = ring.tile([P, cols.stop - cols.start], F32, name="y")
+            for first in range(cols.start, cols.stop, BANK):
+                multiply(n, slice(first, first + BANK), y[:, first - cols.start : first - cols.start + BANK])
+            nc.sync.dma_start(out=out_0[n * P : (n + 1) * P, cols], in_=y[:])
+
+        quantise_chunk(0)
+        quantise_chunk(1)
+        store_codes(slice(0, BANK))
+        quantise_chunk(2)
+        store_codes(chunks[2])
+        quantise_chunk(3)
+        quantise_chunk(4)
+        for n in range(N // P):
+            multiply_and_store(n, slice(0, BANK))
+        store_codes(chunks[3])
+        for n in range(N // P):
+            multiply_and_store(n, slice(BANK, 2 * BANK))
+        store_codes(chunks[4])
+        store_page_plane(slice(0, T2))
+        for n in range(N // P - 1):
+            multiply_and_store(n, slice(2 * BANK, T2))
+        for cols in chunks[-2:]:
+            multiply_and_store(N // P - 1, cols)

@@ -33,6 +33,7 @@ EARLY_SLICES = 2
 RUN = 4
 AHEAD = 2
 BANKS = 8
+Q_BANKS = 4
 FIRST = 256
 WARM = 3
 Y_BUFS = 8
@@ -84,7 +85,7 @@ def tile_list_allergy_archive_kernel(
         nc.sync.dma_start(out=wgs_sb[:], in_=wgs)
         nc.sync.dma_start(pick[:], offs)
         for q in range(QUADS):
-            nc.sync.dma_start(
+            nc.gpsimd.dma_start(
                 out=tab_plane[QUAD * q : QUAD * q + SCALE_ROWS * PASSES, :].bitcast(I32),
                 in_=tab_scales[:, SCALE_ROWS * q : SCALE_ROWS * (q + 1), :].bitcast(I32),
             )
@@ -139,12 +140,12 @@ def tile_list_allergy_archive_kernel(
 
         w1_codes, w1_plane, picked = [], [], []
 
-        def quantise_w1(a):
+        def quantise_w1(a, on_scalar):
             w1_bf = held("w1_bf%d" % a, [P, PACK * H], BF16)
             dealt = w1_bf[:].rearrange("p (t m j) -> p t m j", t=PACK, j=PACK)
             raw = w1_raw[a][:].rearrange("p j (m t) -> p t m j", t=PACK)
-            nc.scalar.activation(out=dealt[:, : PACK // 2], in_=raw[:, : PACK // 2], func=ACT.Copy)
-            nc.vector.tensor_copy(out=dealt[:, PACK // 2 :], in_=raw[:, PACK // 2 :])
+            nc.scalar.activation(out=dealt[:, :on_scalar], in_=raw[:, :on_scalar], func=ACT.Copy)
+            nc.vector.tensor_copy(out=dealt[:, on_scalar:], in_=raw[:, on_scalar:])
             w1_codes.append(held("w1_codes%d" % a, [P, H], U32))
             w1_plane.append(held("w1_plane%d" % a, [P, H], U8))
             nc.vector.quantize_mx(out=w1_codes[a][:].bitcast(FP8X4), scales=w1_plane[a][:], in_=w1_bf[:])
@@ -157,13 +158,13 @@ def tile_list_allergy_archive_kernel(
             for h in range(HALVES):
                 nc.vector.tensor_copy(picked[a][h][:], tab[a][:].indirect(entries(pick, halves[h])))
 
-        quantise_w1(0)
+        quantise_w1(0, 2)
         for t in range(EARLY_SLICES):
             deal_weight(t, held("weight%d" % t, [P, S], F32))
-        picked_plane = held("picked_plane", [P, S], U8)
-        nc.vector.tensor_copy(picked_plane[:], tab_plane[:].indirect(pick[:]))
         gather_words(0)
-        quantise_w1(1)
+        picked_plane = held("picked_plane", [P, S], U8, after="tab0")
+        nc.vector.tensor_copy(picked_plane[:], tab_plane[:].indirect(pick[:]))
+        quantise_w1(1, 3)
         for t in range(EARLY_SLICES, PACK):
             deal_weight(t, reused.tile([P, S], F32, name="weight%d" % t, offset=(t - EARLY_SLICES) * S * 4))
         gather_words(1)
@@ -196,7 +197,7 @@ def tile_list_allergy_archive_kernel(
                 stop=(a == PASSES - 1),
             )
 
-        for i, (t, run) in enumerate(runs[:BANKS]):
+        for i, (t, run) in enumerate(runs[:Q_BANKS]):
             q_sum[t, run.start] = bank(i)[:, : run.stop - run.start]
             first_stage_pass(0, t, run)
 
@@ -206,8 +207,8 @@ def tile_list_allergy_archive_kernel(
                 squares = shared.tile([P, PACK * S + N * PACK // 2], F32, name="squares", offset=0)
             for run in bank_runs(cols):
                 i = runs.index((t, run))
-                if i >= BANKS:
-                    q_sum[t, run.start] = bank(i % BANKS)[:, : run.stop - run.start]
+                if i >= Q_BANKS:
+                    q_sum[t, run.start] = bank(i % Q_BANKS)[:, : run.stop - run.start]
                     first_stage_pass(0, t, run)
                 first_stage_pass(1, t, run)
                 nc.scalar.activation(out=squares[:, run], in_=q_sum[t, run.start], func=ACT.Square)

@@ -26,16 +26,16 @@ BANK = 512
 GROUP = 16
 PASSES = K // (P * PACK)
 HALVES = S // BANK
+BANKS = 8
 WIDTHS = (BANK // 2, BANK // 2, BANK, BANK, BANK)
 CHUNKS = len(WIDTHS)
 BLOCKS = BANK // P
 EARLY_SLICES = 2
 RUN = 4
-AHEAD = 2
-BANKS = 8
+SCALAR_SLICES = (2, 3)
 Q_BANKS = 4
 FIRST = 256
-WARM = 3
+VECTOR_CHUNKS = 3
 Y_BUFS = 8
 
 
@@ -140,7 +140,8 @@ def tile_list_allergy_archive_kernel(
 
         w1_codes, w1_plane, picked = [], [], []
 
-        def quantise_w1(a, on_scalar):
+        def quantise_w1(a):
+            on_scalar = SCALAR_SLICES[a]
             w1_bf = held("w1_bf%d" % a, [P, PACK * H], BF16)
             dealt = w1_bf[:].rearrange("p (t m j) -> p t m j", t=PACK, j=PACK)
             raw = w1_raw[a][:].rearrange("p j (m t) -> p t m j", t=PACK)
@@ -158,13 +159,13 @@ def tile_list_allergy_archive_kernel(
             for h in range(HALVES):
                 nc.vector.tensor_copy(picked[a][h][:], tab[a][:].indirect(entries(pick, halves[h])))
 
-        quantise_w1(0, 2)
+        quantise_w1(0)
         for t in range(EARLY_SLICES):
             deal_weight(t, held("weight%d" % t, [P, S], F32))
         gather_words(0)
         picked_plane = held("picked_plane", [P, S], U8, after="tab0")
         nc.vector.tensor_copy(picked_plane[:], tab_plane[:].indirect(pick[:]))
-        quantise_w1(1, 3)
+        quantise_w1(1)
         for t in range(EARLY_SLICES, PACK):
             deal_weight(t, reused.tile([P, S], F32, name="weight%d" % t, offset=(t - EARLY_SLICES) * S * 4))
         gather_words(1)
@@ -201,10 +202,11 @@ def tile_list_allergy_archive_kernel(
             q_sum[t, run.start] = bank(i)[:, : run.stop - run.start]
             first_stage_pass(0, t, run)
 
+        column_bytes = PACK * 2
+        pairs_bytes, wa_bytes = T2 * column_bytes, N * column_bytes
         feature = [held("feature%d" % t, [P, S], F32) for t in range(PACK)]
         for t, cols in pieces:
-            if True:
-                squares = shared.tile([P, PACK * S + N * PACK // 2], F32, name="squares", offset=0)
+            squares = shared.tile([P, (pairs_bytes + wa_bytes) // 4], F32, name="squares", offset=0)
             for run in bank_runs(cols):
                 i = runs.index((t, run))
                 if i >= Q_BANKS:
@@ -215,7 +217,7 @@ def tile_list_allergy_archive_kernel(
             for run in bank_runs(cols) if cols.stop == FIRST else [cols]:
                 nc.scalar.activation(out=feature[t][:, run], in_=squares[:, run], func=ACT.Exp, scale=-1.0)
 
-        wa_bf = shared.tile([P, N * PACK], BF16, name="wa_bf", offset=PACK * S * 4, align_bytes=64)
+        wa_bf = shared.tile([P, N * PACK], BF16, name="wa_bf", offset=pairs_bytes, align_bytes=64)
         nc.scalar.activation(
             out=wa_bf[:].rearrange("p (c i j) -> p c j i", i=RUN, j=PACK),
             in_=wa_raw[:].rearrange("p (j c i) -> p c j i", i=RUN, j=PACK),
@@ -223,7 +225,6 @@ def tile_list_allergy_archive_kernel(
         )
 
         out_1_rows = out_1.rearrange("(p t) m -> t p m", t=PACK)
-        column_bytes = PACK * 2
         pairs = [
             shared.tile([P, 2, WIDTHS[c], 2], BF16, name="pairs%d" % c, offset=chunks[c].start * column_bytes)
             for c in range(CHUNKS)
@@ -246,26 +247,15 @@ def tile_list_allergy_archive_kernel(
         wa_plane = held("wa_plane", [P, N], U8)
         nc.vector.quantize_mx(out=wa_codes[:].bitcast(FP8X4), scales=wa_plane[:], in_=wa_bf[:])
 
-        for i in range(WARM):
-            nc.tensor.matmul_mx(
-                out=bank(BANKS - 1 - i)[:],
-                lhsT=wa_codes[:, :P].bitcast(FP8X4),
-                lhsT_scale=wa_plane[:, :P],
-                rhs=wa_codes[:].bitcast(FP8X4),
-                rhs_scale=wa_plane[:],
-                start=True,
-                stop=True,
-            )
-
         page_plane = held("page_plane", [P, T2], U8)
         out_2_words = out_2[0].rearrange("p m t -> p (m t)").bitcast(I32)
         page_codes = held("page_codes", [P, T2], U32)
 
         def quantise_chunk(c):
             round_into_pairs(PACK - 1, c)
-            wide = WIDTHS[c] == BANK
-            grouped = held("grouped_wide" if wide else "grouped%d" % c, [P, WIDTHS[c] * PACK], BF16)
-            (nc.gpsimd if c > 2 else nc.vector).tensor_copy(
+            grouped_name = "grouped_wide" if WIDTHS[c] == BANK else "grouped%d" % c
+            grouped = held(grouped_name, [P, WIDTHS[c] * PACK], BF16)
+            (nc.vector if c < VECTOR_CHUNKS else nc.gpsimd).tensor_copy(
                 out=grouped[:].bitcast(I32).rearrange("p (m u) -> p m u", u=2),
                 in_=pairs[c][:].rearrange("p u m e -> p (u m e)").bitcast(I32).rearrange("p (u m) -> p m u", u=2),
             )
@@ -276,19 +266,19 @@ def tile_list_allergy_archive_kernel(
         def store_codes(cols):
             nc.sync.dma_start(out=out_2_words[:, cols], in_=page_codes[:, cols].bitcast(I32))
 
-        def store_page_plane(cols):
+        def store_page_plane():
             for q in range(QUADS):
                 nc.sync.dma_start(
-                    out=out_3[0, SCALE_ROWS * q : SCALE_ROWS * (q + 1), cols].bitcast(I32),
-                    in_=page_plane[QUAD * q : QUAD * q + SCALE_ROWS, cols].bitcast(I32),
+                    out=out_3[0, SCALE_ROWS * q : SCALE_ROWS * (q + 1), :].bitcast(I32),
+                    in_=page_plane[QUAD * q : QUAD * q + SCALE_ROWS, :].bitcast(I32),
                 )
 
-        done = []
+        made = []
 
         def multiply(n, cols, y):
             rows = slice(n * P, (n + 1) * P)
-            first = 2 * len(done) % BANKS
-            done.append((n, cols))
+            first = 2 * len(made) % BANKS
+            made.append(y)
             a_sum, b_sum = bank(first), bank(first + 1)
             nc.tensor.matmul_mx(
                 out=a_sum[:],
@@ -313,25 +303,27 @@ def tile_list_allergy_archive_kernel(
 
         def multiply_and_store(n, cols):
             y = ring.tile([P, cols.stop - cols.start], F32, name="y")
-            for first in range(cols.start, cols.stop, BANK):
-                multiply(n, slice(first, first + BANK), y[:, first - cols.start : first - cols.start + BANK])
+            for m0 in range(cols.start, cols.stop, BANK):
+                multiply(n, slice(m0, m0 + BANK), y[:, m0 - cols.start : m0 - cols.start + BANK])
             nc.sync.dma_start(out=out_0[n * P : (n + 1) * P, cols], in_=y[:])
 
+        quarters = [slice(m0, m0 + BANK) for m0 in range(0, T2, BANK)]
+        row_blocks = range(N // P)
         quantise_chunk(0)
         quantise_chunk(1)
-        store_codes(slice(0, BANK))
+        store_codes(quarters[0])
         quantise_chunk(2)
-        store_codes(chunks[2])
+        store_codes(quarters[1])
         quantise_chunk(3)
         quantise_chunk(4)
-        for n in range(N // P):
-            multiply_and_store(n, slice(0, BANK))
-        store_codes(chunks[3])
-        for n in range(N // P):
-            multiply_and_store(n, slice(BANK, 2 * BANK))
-        store_codes(chunks[4])
-        store_page_plane(slice(0, T2))
-        for n in range(N // P - 1):
-            multiply_and_store(n, slice(2 * BANK, T2))
-        for cols in chunks[-2:]:
-            multiply_and_store(N // P - 1, cols)
+        for n in row_blocks:
+            multiply_and_store(n, quarters[0])
+        store_codes(quarters[2])
+        for n in row_blocks:
+            multiply_and_store(n, quarters[1])
+        store_codes(quarters[3])
+        store_page_plane()
+        for n in row_blocks[:-1]:
+            multiply_and_store(n, slice(quarters[2].start, quarters[3].stop))
+        for cols in quarters[2:]:
+            multiply_and_store(row_blocks[-1], cols)

@@ -22,7 +22,9 @@ PACK = 4
 QUAD = 32
 QUADS = P // QUAD
 SCALE_ROWS = 4
+PASSES_ROWS = K // 32
 BANK = 512
+ROW_STEP = P // (PASSES_ROWS)
 GROUP = 16
 PASSES = K // (P * PACK)
 HALVES = S // BANK
@@ -64,9 +66,11 @@ def tile_list_allergy_archive_kernel(
         pick = lists.tile([P, S // GROUP], U16, name="pick")
         place = lists.tile([P, S // GROUP], U16, name="place")
 
-        tab_plane = held("tab_plane", [P, T], U8)
+        tab_rows = held("tab_rows", [P, T], U8)
+        picked_plane = held("picked_plane", [P, S], U8)
         wb_plane = held("wb_plane", [P, N], U8)
-        nc.vector.memset(tab_plane[:].bitcast(I32), 0)
+        nc.vector.memset(tab_rows[:].bitcast(I32), 0)
+        nc.vector.memset(picked_plane[:].bitcast(I32), 0)
         nc.vector.memset(wb_plane[:].bitcast(I32), 0)
 
         def load_w1(a):
@@ -84,11 +88,9 @@ def tile_list_allergy_archive_kernel(
         gain_sb = held("gain_sb", [P, PACK], F32)
         nc.sync.dma_start(out=wgs_sb[:], in_=wgs)
         nc.sync.dma_start(pick[:], offs)
-        for q in range(QUADS):
-            nc.gpsimd.dma_start(
-                out=tab_plane[QUAD * q : QUAD * q + SCALE_ROWS * PASSES, :].bitcast(I32),
-                in_=tab_scales[:, SCALE_ROWS * q : SCALE_ROWS * (q + 1), :].bitcast(I32),
-            )
+        nc.sync.dma_start(
+            out=tab_rows[0:P:ROW_STEP, :].bitcast(I32), in_=tab_scales.rearrange("a q n -> (a q) n").bitcast(I32)
+        )
         load_w1(0)
         nc.sync.dma_start(out=gain_sb[:], in_=gain.rearrange("(p t) -> p t", t=PACK))
         load_tab(0)
@@ -159,12 +161,20 @@ def tile_list_allergy_archive_kernel(
             for h in range(HALVES):
                 nc.vector.tensor_copy(picked[a][h][:], tab[a][:].indirect(entries(pick, halves[h])))
 
+        picked_rows = held("picked_rows", [P, S], U8)
+        nc.vector.tensor_copy(picked_rows[:], tab_rows[:].indirect(pick[:]))
+        for a in range(PASSES):
+            for q in range(QUADS):
+                first = ROW_STEP * SCALE_ROWS * (QUADS * a + q)
+                to = QUAD * q + SCALE_ROWS * a
+                nc.gpsimd.dma_start(
+                    out=picked_plane[to : to + SCALE_ROWS, :].bitcast(I32),
+                    in_=picked_rows[first : first + ROW_STEP * SCALE_ROWS : ROW_STEP, :].bitcast(I32),
+                )
         quantise_w1(0)
         for t in range(EARLY_SLICES):
             deal_weight(t, held("weight%d" % t, [P, S], F32))
         gather_words(0)
-        picked_plane = held("picked_plane", [P, S], U8, after="tab0")
-        nc.vector.tensor_copy(picked_plane[:], tab_plane[:].indirect(pick[:]))
         quantise_w1(1)
         for t in range(EARLY_SLICES, PACK):
             deal_weight(t, reused.tile([P, S], F32, name="weight%d" % t, offset=(t - EARLY_SLICES) * S * 4))

@@ -37,8 +37,8 @@ RUN = 4
 SCALAR_SLICES = (2, 3)
 Q_BANKS = 4
 FIRST = 256
-VECTOR_CHUNKS = 3
-Y_BUFS = 8
+VECTOR_CHUNKS = 4
+Y_BUFS = 7
 
 
 def tile_list_allergy_archive_kernel(
@@ -263,11 +263,10 @@ def tile_list_allergy_archive_kernel(
 
         def quantise_chunk(c):
             round_into_pairs(PACK - 1, c)
-            grouped_name = "grouped_wide" if WIDTHS[c] == BANK else "grouped%d" % c
-            grouped = held(grouped_name, [P, WIDTHS[c] * PACK], BF16)
-            (nc.vector if c < VECTOR_CHUNKS else nc.gpsimd).tensor_copy(
-                out=grouped[:].bitcast(I32).rearrange("p (m u) -> p m u", u=2),
-                in_=pairs[c][:].rearrange("p u m e -> p (u m e)").bitcast(I32).rearrange("p (u m) -> p m u", u=2),
+            grouped = held("grouped%d" % c, [P, WIDTHS[c] * PACK], BF16)
+            (nc.vector.tensor_copy if c < VECTOR_CHUNKS else nc.scalar.copy)(
+                out=grouped[:].bitcast(U32).rearrange("p (m u) -> p m u", u=2),
+                in_=pairs[c][:].rearrange("p u m e -> p (u m e)").bitcast(U32).rearrange("p (u m) -> p m u", u=2),
             )
             nc.vector.quantize_mx(
                 out=page_codes[:, chunks[c]].bitcast(FP8X4), scales=page_plane[:, chunks[c]], in_=grouped[:]
@@ -318,22 +317,20 @@ def tile_list_allergy_archive_kernel(
             nc.sync.dma_start(out=out_0[n * P : (n + 1) * P, cols], in_=y[:])
 
         quarters = [slice(m0, m0 + BANK) for m0 in range(0, T2, BANK)]
+        page_halves = [slice(m0, m0 + 2 * BANK) for m0 in range(0, T2, 2 * BANK)]
         row_blocks = range(N // P)
         quantise_chunk(0)
         quantise_chunk(1)
         store_codes(quarters[0])
-        quantise_chunk(2)
-        store_codes(quarters[1])
-        quantise_chunk(3)
-        quantise_chunk(4)
-        for n in row_blocks:
-            multiply_and_store(n, quarters[0])
-        store_codes(quarters[2])
-        for n in row_blocks:
-            multiply_and_store(n, quarters[1])
-        store_codes(quarters[3])
+        for c in range(2, CHUNKS):
+            quantise_chunk(c)
+            store_codes(chunks[c])
         store_page_plane()
+        for cols in quarters[:2]:
+            multiply_and_store(row_blocks[0], cols)
+        for n in row_blocks[1:]:
+            multiply_and_store(n, page_halves[0])
         for n in row_blocks[:-1]:
-            multiply_and_store(n, slice(quarters[2].start, quarters[3].stop))
+            multiply_and_store(n, page_halves[1])
         for cols in quarters[2:]:
             multiply_and_store(row_blocks[-1], cols)

@@ -277,7 +277,7 @@ def tile_list_allergy_archive_kernel(
 
         def store_page_plane():
             for q in range(QUADS):
-                nc.sync.dma_start(
+                nc.gpsimd.dma_start(
                     out=out_3[0, SCALE_ROWS * q : SCALE_ROWS * (q + 1), :].bitcast(I32),
                     in_=page_plane[QUAD * q : QUAD * q + SCALE_ROWS, :].bitcast(I32),
                 )

@@ -34,7 +34,7 @@ CHUNKS = len(WIDTHS)
 BLOCKS = BANK // P
 EARLY_SLICES = 2
 RUN = 4
-SCALAR_SLICES = (2, 3)
+SCALAR_SLICES = (4, 3)
 Q_BANKS = 4
 FIRST = 256
 VECTOR_CHUNKS = 4
@@ -130,15 +130,17 @@ def tile_list_allergy_archive_kernel(
 
         weight = []
 
-        def deal_weight(t, tile):
+        def deal_weight(t, tile, on_vector):
             weight.append(tile)
             for h in range(HALVES):
                 back = bank(HALVES * t + h)
                 for g in range(BLOCKS):
                     nc.tensor.transpose(back[:, g * P : (g + 1) * P], spread[:, h, g, t, :], identity[:])
-                nc.scalar.activation(
-                    out=tile[:, halves[h]], in_=back[:], func=ACT.Copy, scale=gain_sb[:, t : t + 1]
-                )
+                out, factor = tile[:, halves[h]], gain_sb[:, t : t + 1]
+                if on_vector:
+                    nc.vector.tensor_scalar(out=out, in0=back[:], scalar1=factor, scalar2=None, op0=ALU.mult)
+                else:
+                    nc.scalar.activation(out=out, in_=back[:], func=ACT.Copy, scale=factor)
 
         w1_codes, w1_plane, picked = [], [], []
 
@@ -148,7 +150,8 @@ def tile_list_allergy_archive_kernel(
             dealt = w1_bf[:].rearrange("p (t m j) -> p t m j", t=PACK, j=PACK)
             raw = w1_raw[a][:].rearrange("p j (m t) -> p t m j", t=PACK)
             nc.scalar.activation(out=dealt[:, :on_scalar], in_=raw[:, :on_scalar], func=ACT.Copy)
-            nc.vector.tensor_copy(out=dealt[:, on_scalar:], in_=raw[:, on_scalar:])
+            if on_scalar < PACK:
+                nc.vector.tensor_copy(out=dealt[:, on_scalar:], in_=raw[:, on_scalar:])
             w1_codes.append(held("w1_codes%d" % a, [P, H], U32))
             w1_plane.append(held("w1_plane%d" % a, [P, H], U8))
             nc.vector.quantize_mx(out=w1_codes[a][:].bitcast(FP8X4), scales=w1_plane[a][:], in_=w1_bf[:])
@@ -171,13 +174,13 @@ def tile_list_allergy_archive_kernel(
                     out=picked_plane[to : to + SCALE_ROWS, :].bitcast(I32),
                     in_=picked_rows[first : first + ROW_STEP * SCALE_ROWS : ROW_STEP, :].bitcast(I32),
                 )
-        quantise_w1(0)
         for t in range(EARLY_SLICES):
-            deal_weight(t, held("weight%d" % t, [P, S], F32))
+            deal_weight(t, held("weight%d" % t, [P, S], F32), on_vector=True)
         gather_words(0)
+        quantise_w1(0)
         quantise_w1(1)
         for t in range(EARLY_SLICES, PACK):
-            deal_weight(t, reused.tile([P, S], F32, name="weight%d" % t, offset=(t - EARLY_SLICES) * S * 4))
+            deal_weight(t, reused.tile([P, S], F32, name="weight%d" % t, offset=(t - EARLY_SLICES) * S * 4), on_vector=False)
         gather_words(1)
 
         pieces = [(0, slice(0, FIRST)), (1, halves[0]), (0, slice(FIRST, S)), (1, halves[1])]

@@ -152,7 +152,7 @@ def tile_list_allergy_archive_kernel(
             nc.scalar.activation(out=dealt[:, :on_scalar], in_=raw[:, :on_scalar], func=ACT.Copy)
             if on_scalar < PACK:
                 nc.vector.tensor_copy(out=dealt[:, on_scalar:], in_=raw[:, on_scalar:])
-            w1_codes.append(held("w1_codes%d" % a, [P, H], U32))
+            w1_codes.append(held("w1_codes%d" % a, [P, H], U32, after="tab0" if a == 0 else None))
             w1_plane.append(held("w1_plane%d" % a, [P, H], U8))
             nc.vector.quantize_mx(out=w1_codes[a][:].bitcast(FP8X4), scales=w1_plane[a][:], in_=w1_bf[:])
 

@@ -18,13 +18,14 @@ ACT = mybir.ActivationFunctionType
 ALU = mybir.AluOpType
 
 P = 128
+KIB = 1024
 PACK = 4
 QUAD = 32
 QUADS = P // QUAD
 SCALE_ROWS = 4
-PASSES_ROWS = K // 32
+TAB_SCALE_ROWS = K // 32
 BANK = 512
-ROW_STEP = P // (PASSES_ROWS)
+ROW_STEP = P // TAB_SCALE_ROWS
 GROUP = 16
 PASSES = K // (P * PACK)
 HALVES = S // BANK
@@ -32,9 +33,8 @@ BANKS = 8
 WIDTHS = (BANK // 2, BANK // 2, BANK, BANK, BANK)
 CHUNKS = len(WIDTHS)
 BLOCKS = BANK // P
-EARLY_SLICES = 2
+EARLY = 2
 RUN = 4
-SCALAR_SLICES = (4, 3)
 Q_BANKS = 4
 FIRST = 256
 VECTOR_CHUNKS = 4
@@ -49,139 +49,137 @@ def tile_list_allergy_archive_kernel(
     with ExitStack() as ctx:
         lists = ctx.enter_context(tc.tile_pool(name="lists", bufs=1))
         keep = ctx.enter_context(tc.tile_pool(name="keep", bufs=1))
-        shared = ctx.enter_context(tc.tile_pool(name="shared", bufs=1))
-        reused = ctx.enter_context(tc.tile_pool(name="reused", bufs=1))
+        loads = ctx.enter_context(tc.tile_pool(name="loads", bufs=1))
         ring = ctx.enter_context(tc.tile_pool(name="ring", bufs=Y_BUFS))
         psum = ctx.enter_context(tc.psum_pool(name="psum", bufs=1))
 
         def held(name, shape, dtype, after=None):
             return keep.tile(shape, dtype, name=name, tag=after or name, align_bytes=64)
 
+        def placed(name, shape, dtype, kib):
+            return loads.tile(shape, dtype, name=name, offset=int(kib * KIB), align_bytes=64)
+
         def bank(i):
             return psum.tile([P, BANK], F32, name="bank%d" % i)
 
+        def entries(offsets, cols):
+            return offsets[:, cols.start // GROUP : cols.stop // GROUP]
+
         halves = [slice(h * BANK, (h + 1) * BANK) for h in range(HALVES)]
         chunks = [slice(sum(WIDTHS[:c]), sum(WIDTHS[: c + 1])) for c in range(CHUNKS)]
+        page_rows = page0.rearrange("(p t) m -> t p m", t=PACK)
+        wgs_rows = wgs.rearrange("(i t) j -> i (t j)", t=PACK)
 
         pick = lists.tile([P, S // GROUP], U16, name="pick")
         place = lists.tile([P, S // GROUP], U16, name="place")
-
-        tab_rows = held("tab_rows", [P, T], U8)
+        tab_rows = placed("tab_rows", [P, T], U8, 75)
         picked_plane = held("picked_plane", [P, S], U8)
-        wb_plane = held("wb_plane", [P, N], U8)
         nc.vector.memset(tab_rows[:].bitcast(I32), 0)
         nc.vector.memset(picked_plane[:].bitcast(I32), 0)
-        nc.vector.memset(wb_plane[:].bitcast(I32), 0)
+
+        wgs_early = held("wgs_early", [P, BANK], F32)
+        w1_raw = [held("w1_raw%d" % a, [P, PACK, H], F32) for a in range(PASSES)]
+        gain_sb = held("gain_sb", [P, PACK], F32)
+        tab = [placed("tab0", [P, T], U32, 4)]
 
         def load_w1(a):
             rows = w1[a * P * PACK : (a + 1) * P * PACK, :]
             nc.sync.dma_start(out=w1_raw[a][:], in_=rows.rearrange("(p j) c -> p j c", j=PACK))
 
-        def load_tab(a):
-            nc.sync.dma_start(
-                out=tab[a][:].bitcast(I32), in_=tab_words[a].rearrange("p n t -> p (n t)").bitcast(I32)
-            )
+        def load_tab(a, cols):
+            words = tab_words[a].rearrange("p n t -> p (n t)").bitcast(I32)
+            nc.sync.dma_start(out=tab[a][:, cols].bitcast(I32), in_=words[:, cols])
 
-        w1_raw = [held("w1_raw0", [P, PACK, H], F32), reused.tile([P, PACK, H], F32, name="w1_raw1", offset=0)]
-        tab = [held("tab%d" % a, [P, T], U32) for a in range(PASSES)]
-        wgs_sb = held("wgs_sb", [P, S], F32)
-        gain_sb = held("gain_sb", [P, PACK], F32)
-        nc.sync.dma_start(out=wgs_sb[:], in_=wgs)
+        nc.sync.dma_start(out=wgs_early[:], in_=wgs_rows[:, : EARLY * S].rearrange("i (k c) -> i k c", c=BANK))
         nc.sync.dma_start(pick[:], offs)
         nc.sync.dma_start(
             out=tab_rows[0:P:ROW_STEP, :].bitcast(I32), in_=tab_scales.rearrange("a q n -> (a q) n").bitcast(I32)
         )
         load_w1(0)
         nc.sync.dma_start(out=gain_sb[:], in_=gain.rearrange("(p t) -> p t", t=PACK))
-        load_tab(0)
-        load_w1(1)
         nc.sync.dma_start(place[:], offs2)
-        load_tab(1)
+        load_w1(1)
+        load_tab(0, slice(0, T))
 
-        page_rows = page0.rearrange("(p t) m -> t p m", t=PACK)
-        page = [held("page%d" % t, [P, T2], F32) for t in range(PACK)]
-        wa_raw = held("wa_raw", [P, PACK * N], F32)
+        picked_rows = held("picked_rows", [P, S], U8)
+        nc.vector.tensor_copy(picked_rows[:], tab_rows[:].indirect(pick[:]))
+        tab.append(placed("tab1", [P, T], U32, 60))
+        for a in range(PASSES):
+            for q in range(QUADS):
+                first = ROW_STEP * SCALE_ROWS * (QUADS * a + q)
+                to = QUAD * q + SCALE_ROWS * a
+                nc.sync.dma_start(
+                    out=picked_plane[to : to + SCALE_ROWS, :].bitcast(I32),
+                    in_=picked_rows[first : first + ROW_STEP * SCALE_ROWS : ROW_STEP, :].bitcast(I32),
+                )
+            load_tab(1, slice(a * T // PASSES, (a + 1) * T // PASSES))
+        page = [placed("page0", [P, T2], F32, 76)]
         nc.sync.dma_start(out=page[0][:], in_=page_rows[0])
-        nc.sync.dma_start(out=page[1][:], in_=page_rows[1])
-        nc.sync.dma_start(out=wa_raw[:], in_=wa.rearrange("(p j) n -> p (j n)", j=PACK))
-        nc.sync.dma_start(out=page[2][:], in_=page_rows[2])
-        nc.sync.dma_start(out=page[3][:], in_=page_rows[3])
-        wb_codes = held("wb_codes", [P, 2 * N], U8)
-        nc.sync.dma_start(out=wb_codes[:].bitcast(I32), in_=wb_words[0].bitcast(I32))
-        for q in range(QUADS):
-            nc.sync.dma_start(
-                out=wb_plane[QUAD * q : QUAD * q + SCALE_ROWS, :].bitcast(I32),
-                in_=wb_scales[0, SCALE_ROWS * q : SCALE_ROWS * (q + 1), :].bitcast(I32),
-            )
 
         identity = held("identity", [P, P], F32)
         make_identity(nc, identity[:])
-        spread = shared.tile([P, HALVES, BLOCKS, PACK, P], F32, name="spread", offset=0)
-        for h, copy_out in enumerate((nc.scalar.copy, nc.vector.tensor_copy)):
-            turned = bank(HALVES * (PACK - 1) + h)
-            for g in range(BLOCKS):
-                j0 = h * BANK + g * P
-                nc.tensor.transpose(turned[:, g * P : (g + 1) * P], wgs_sb[:, j0 : j0 + P], identity[:])
-            by_slice = turned[:].rearrange("p (g i t) -> p g t i", g=BLOCKS, t=PACK)
-            copy_out(
+        spread = placed("spread", [P, HALVES, BLOCKS, EARLY, P], F32, 24)
+        turned = bank(BANKS - 1)
+        for g in range(BLOCKS):
+            nc.tensor.transpose(turned[:, g * P : (g + 1) * P], wgs_early[:, g * P : (g + 1) * P], identity[:])
+        by_half = turned[:].rearrange("p (g i t h) -> p h g t i", g=BLOCKS, t=EARLY, h=HALVES)
+        for h in range(HALVES):
+            nc.scalar.copy(
                 out=spread[:, h].rearrange("p g t (q i) -> p g t q i", i=QUAD),
-                in_=by_slice.unsqueeze(3).to_broadcast([P, BLOCKS, PACK, QUADS, QUAD]),
+                in_=by_half[:, h].unsqueeze(3).to_broadcast([P, BLOCKS, EARLY, QUADS, QUAD]),
             )
-
         weight = []
-
-        def deal_weight(t, tile, on_vector):
-            weight.append(tile)
+        for t in range(EARLY):
+            weight.append(held("weight%d" % t, [P, S], F32))
             for h in range(HALVES):
                 back = bank(HALVES * t + h)
                 for g in range(BLOCKS):
                     nc.tensor.transpose(back[:, g * P : (g + 1) * P], spread[:, h, g, t, :], identity[:])
-                out, factor = tile[:, halves[h]], gain_sb[:, t : t + 1]
-                if on_vector:
-                    nc.vector.tensor_scalar(out=out, in0=back[:], scalar1=factor, scalar2=None, op0=ALU.mult)
-                else:
-                    nc.scalar.activation(out=out, in_=back[:], func=ACT.Copy, scale=factor)
+                nc.vector.tensor_scalar(
+                    out=weight[t][:, halves[h]], in0=back[:], scalar1=gain_sb[:, t : t + 1], scalar2=None, op0=ALU.mult
+                )
 
         w1_codes, w1_plane, picked = [], [], []
-
-        def quantise_w1(a):
-            on_scalar = SCALAR_SLICES[a]
+        for a, engine_copy in enumerate((nc.scalar.copy, nc.vector.tensor_copy)):
             w1_bf = held("w1_bf%d" % a, [P, PACK * H], BF16)
-            dealt = w1_bf[:].rearrange("p (t m j) -> p t m j", t=PACK, j=PACK)
-            raw = w1_raw[a][:].rearrange("p j (m t) -> p t m j", t=PACK)
-            nc.scalar.activation(out=dealt[:, :on_scalar], in_=raw[:, :on_scalar], func=ACT.Copy)
-            if on_scalar < PACK:
-                nc.vector.tensor_copy(out=dealt[:, on_scalar:], in_=raw[:, on_scalar:])
-            w1_codes.append(held("w1_codes%d" % a, [P, H], U32, after="tab0" if a == 0 else None))
+            engine_copy(
+                out=w1_bf[:].rearrange("p (t m j) -> p m t j", t=PACK, j=PACK),
+                in_=w1_raw[a][:].rearrange("p j (m t) -> p m t j", t=PACK),
+            )
+            w1_codes.append(held("w1_codes%d" % a, [P, H], U32))
             w1_plane.append(held("w1_plane%d" % a, [P, H], U8))
             nc.vector.quantize_mx(out=w1_codes[a][:].bitcast(FP8X4), scales=w1_plane[a][:], in_=w1_bf[:])
-
-        def entries(offsets, cols):
-            return offsets[:, cols.start // GROUP : cols.stop // GROUP]
 
         def gather_words(a):
             picked.append([held("picked%d_%d" % (a, h), [P, BANK], U32) for h in range(HALVES)])
             for h in range(HALVES):
                 nc.vector.tensor_copy(picked[a][h][:], tab[a][:].indirect(entries(pick, halves[h])))
 
-        picked_rows = held("picked_rows", [P, S], U8)
-        nc.vector.tensor_copy(picked_rows[:], tab_rows[:].indirect(pick[:]))
-        for a in range(PASSES):
-            for q in range(QUADS):
-                first = ROW_STEP * SCALE_ROWS * (QUADS * a + q)
-                to = QUAD * q + SCALE_ROWS * a
-                nc.gpsimd.dma_start(
-                    out=picked_plane[to : to + SCALE_ROWS, :].bitcast(I32),
-                    in_=picked_rows[first : first + ROW_STEP * SCALE_ROWS : ROW_STEP, :].bitcast(I32),
-                )
-        for t in range(EARLY_SLICES):
-            deal_weight(t, held("weight%d" % t, [P, S], F32), on_vector=True)
         gather_words(0)
-        quantise_w1(0)
-        quantise_w1(1)
-        for t in range(EARLY_SLICES, PACK):
-            deal_weight(t, reused.tile([P, S], F32, name="weight%d" % t, offset=(t - EARLY_SLICES) * S * 4), on_vector=False)
+        page.append(placed("page1", [P, T2], F32, 0))
+        nc.sync.dma_start(out=page[1][:], in_=page_rows[1])
+        wgs_late = placed("wgs_late", [P, PACK - EARLY, S], F32, 16)
+        for q in range(QUADS):
+            nc.sync.dma_start(
+                out=wgs_late[QUAD * q : QUAD * (q + 1)].rearrange("p t j -> p (t j)"), in_=wgs_rows[:, EARLY * S :]
+            )
+        wa_raw = placed("wa_raw", [P, PACK * N], F32, 8)
+        nc.sync.dma_start(out=wa_raw[:], in_=wa.rearrange("(p j) n -> p (j n)", j=PACK))
+
         gather_words(1)
+        page.append(placed("page2", [P, T2], F32, 56))
+        page.append(placed("page3", [P, T2], F32, 66))
+        for t in range(2, PACK):
+            nc.sync.dma_start(out=page[t][:], in_=page_rows[t])
+        wb_codes = placed("wb_codes", [P, 2 * N], U8, 64)
+        wb_plane = placed("wb_plane", [P, N], U8, 65)
+        nc.sync.dma_start(out=wb_codes[:].bitcast(I32), in_=wb_words[0].bitcast(I32))
+        nc.gpsimd.memset(wb_plane[:].bitcast(I32), 0)
+        for q in range(QUADS):
+            nc.sync.dma_start(
+                out=wb_plane[QUAD * q : QUAD * q + SCALE_ROWS, :].bitcast(I32),
+                in_=wb_scales[0, SCALE_ROWS * q : SCALE_ROWS * (q + 1), :].bitcast(I32),
+            )
 
         pieces = [(0, slice(0, FIRST)), (1, halves[0]), (0, slice(FIRST, S)), (1, halves[1])]
         pieces.extend((t, slice(0, S)) for t in range(2, PACK))
@@ -216,10 +214,21 @@ def tile_list_allergy_archive_kernel(
             first_stage_pass(0, t, run)
 
         column_bytes = PACK * 2
-        pairs_bytes, wa_bytes = T2 * column_bytes, N * column_bytes
         feature = [held("feature%d" % t, [P, S], F32) for t in range(PACK)]
+
+        def late_weights():
+            for t in range(EARLY, PACK):
+                weight.append(placed("weight%d" % t, [P, S], F32, 48 + 4 * (t - EARLY)))
+                nc.scalar.activation(
+                    out=weight[t][:], in_=wgs_late[:, t - EARLY, :], func=ACT.Copy, scale=gain_sb[:, t : t + 1]
+                )
+
         for t, cols in pieces:
-            squares = shared.tile([P, (pairs_bytes + wa_bytes) // 4], F32, name="squares", offset=0)
+            if t < PACK - 1:
+                squares = placed("squares", [P, 32 * KIB // 4], F32, 24)
+            else:
+                late_weights()
+                squares = placed("last_squares", [P, 25 * KIB // 4], F32, 23)[:, KIB // 4 :]
             for run in bank_runs(cols):
                 i = runs.index((t, run))
                 if i >= Q_BANKS:
@@ -230,7 +239,7 @@ def tile_list_allergy_archive_kernel(
             for run in bank_runs(cols) if cols.stop == FIRST else [cols]:
                 nc.scalar.activation(out=feature[t][:, run], in_=squares[:, run], func=ACT.Exp, scale=-1.0)
 
-        wa_bf = shared.tile([P, N * PACK], BF16, name="wa_bf", offset=pairs_bytes, align_bytes=64)
+        wa_bf = placed("wa_bf", [P, N * PACK], BF16, 28)
         nc.scalar.activation(
             out=wa_bf[:].rearrange("p (c i j) -> p c j i", i=RUN, j=PACK),
             in_=wa_raw[:].rearrange("p (j c i) -> p c j i", i=RUN, j=PACK),
@@ -239,7 +248,7 @@ def tile_list_allergy_archive_kernel(
 
         out_1_rows = out_1.rearrange("(p t) m -> t p m", t=PACK)
         pairs = [
-            shared.tile([P, 2, WIDTHS[c], 2], BF16, name="pairs%d" % c, offset=chunks[c].start * column_bytes)
+            placed("pairs%d" % c, [P, 2, WIDTHS[c], 2], BF16, 32 + chunks[c].start * column_bytes // KIB)
             for c in range(CHUNKS)
         ]
 

@@ -33,7 +33,6 @@ BANKS = 8
 WIDTHS = (BANK // 2, BANK // 2, BANK, BANK, BANK)
 CHUNKS = len(WIDTHS)
 BLOCKS = BANK // P
-EARLY = 2
 RUN = 4
 Q_BANKS = 4
 FIRST = 256
@@ -68,7 +67,6 @@ def tile_list_allergy_archive_kernel(
         halves = [slice(h * BANK, (h + 1) * BANK) for h in range(HALVES)]
         chunks = [slice(sum(WIDTHS[:c]), sum(WIDTHS[: c + 1])) for c in range(CHUNKS)]
         page_rows = page0.rearrange("(p t) m -> t p m", t=PACK)
-        wgs_rows = wgs.rearrange("(i t) j -> i (t j)", t=PACK)
 
         pick = lists.tile([P, S // GROUP], U16, name="pick")
         place = lists.tile([P, S // GROUP], U16, name="place")
@@ -77,7 +75,7 @@ def tile_list_allergy_archive_kernel(
         nc.vector.memset(tab_rows[:].bitcast(I32), 0)
         nc.vector.memset(picked_plane[:].bitcast(I32), 0)
 
-        wgs_early = held("wgs_early", [P, BANK], F32)
+        wgs_sb = held("wgs_sb", [P, S], F32)
         w1_raw = [held("w1_raw%d" % a, [P, PACK, H], F32) for a in range(PASSES)]
         gain_sb = held("gain_sb", [P, PACK], F32)
         tab = [placed("tab0", [P, T], U32, 4)]
@@ -90,7 +88,7 @@ def tile_list_allergy_archive_kernel(
             words = tab_words[a].rearrange("p n t -> p (n t)").bitcast(I32)
             nc.sync.dma_start(out=tab[a][:, cols].bitcast(I32), in_=words[:, cols])
 
-        nc.sync.dma_start(out=wgs_early[:], in_=wgs_rows[:, : EARLY * S].rearrange("i (k c) -> i k c", c=BANK))
+        nc.sync.dma_start(out=wgs_sb[:], in_=wgs)
         nc.sync.dma_start(pick[:], offs)
         nc.sync.dma_start(
             out=tab_rows[0:P:ROW_STEP, :].bitcast(I32), in_=tab_scales.rearrange("a q n -> (a q) n").bitcast(I32)
@@ -118,26 +116,29 @@ def tile_list_allergy_archive_kernel(
 
         identity = held("identity", [P, P], F32)
         make_identity(nc, identity[:])
-        spread = placed("spread", [P, HALVES, BLOCKS, EARLY, P], F32, 24)
-        turned = bank(BANKS - 1)
-        for g in range(BLOCKS):
-            nc.tensor.transpose(turned[:, g * P : (g + 1) * P], wgs_early[:, g * P : (g + 1) * P], identity[:])
-        by_half = turned[:].rearrange("p (g i t h) -> p h g t i", g=BLOCKS, t=EARLY, h=HALVES)
-        for h in range(HALVES):
-            nc.scalar.copy(
+        spread = placed("spread", [P, HALVES, BLOCKS, PACK, P], F32, 24)
+        for h, copy_out in enumerate((nc.scalar.copy, nc.vector.tensor_copy)):
+            turned = bank(HALVES * (PACK - 1) + h)
+            for g in range(BLOCKS):
+                j0 = h * BANK + g * P
+                nc.tensor.transpose(turned[:, g * P : (g + 1) * P], wgs_sb[:, j0 : j0 + P], identity[:])
+            by_slice = turned[:].rearrange("p (g i t) -> p g t i", g=BLOCKS, t=PACK)
+            copy_out(
                 out=spread[:, h].rearrange("p g t (q i) -> p g t q i", i=QUAD),
-                in_=by_half[:, h].unsqueeze(3).to_broadcast([P, BLOCKS, EARLY, QUADS, QUAD]),
+                in_=by_slice.unsqueeze(3).to_broadcast([P, BLOCKS, PACK, QUADS, QUAD]),
             )
         weight = []
-        for t in range(EARLY):
+        for t in range(PACK):
             weight.append(held("weight%d" % t, [P, S], F32))
             for h in range(HALVES):
                 back = bank(HALVES * t + h)
                 for g in range(BLOCKS):
                     nc.tensor.transpose(back[:, g * P : (g + 1) * P], spread[:, h, g, t, :], identity[:])
-                nc.vector.tensor_scalar(
-                    out=weight[t][:, halves[h]], in0=back[:], scalar1=gain_sb[:, t : t + 1], scalar2=None, op0=ALU.mult
-                )
+                out, factor = weight[t][:, halves[h]], gain_sb[:, t : t + 1]
+                if t < 2:
+                    nc.vector.tensor_scalar(out=out, in0=back[:], scalar1=factor, scalar2=None, op0=ALU.mult)
+                else:
+                    nc.scalar.activation(out=out, in_=back[:], func=ACT.Copy, scale=factor)
 
         w1_codes, w1_plane, picked = [], [], []
         for a, engine_copy in enumerate((nc.scalar.copy, nc.vector.tensor_copy)):
@@ -152,17 +153,16 @@ def tile_list_allergy_archive_kernel(
 
         def gather_words(a):
             picked.append([held("picked%d_%d" % (a, h), [P, BANK], U32) for h in range(HALVES)])
-            for h in range(HALVES):
-                nc.vector.tensor_copy(picked[a][h][:], tab[a][:].indirect(entries(pick, halves[h])))
+            cuts = halves if a < PASSES - 1 else [slice(0, FIRST), slice(FIRST, BANK), halves[1]]
+            for cols in cuts:
+                h = cols.start // BANK
+                nc.vector.tensor_copy(
+                    picked[a][h][:, cols.start - h * BANK : cols.stop - h * BANK], tab[a][:].indirect(entries(pick, cols))
+                )
 
         gather_words(0)
         page.append(placed("page1", [P, T2], F32, 0))
         nc.sync.dma_start(out=page[1][:], in_=page_rows[1])
-        wgs_late = placed("wgs_late", [P, PACK - EARLY, S], F32, 16)
-        for q in range(QUADS):
-            nc.sync.dma_start(
-                out=wgs_late[QUAD * q : QUAD * (q + 1)].rearrange("p t j -> p (t j)"), in_=wgs_rows[:, EARLY * S :]
-            )
         wa_raw = placed("wa_raw", [P, PACK * N], F32, 8)
         nc.sync.dma_start(out=wa_raw[:], in_=wa.rearrange("(p j) n -> p (j n)", j=PACK))
 
@@ -215,20 +215,8 @@ def tile_list_allergy_archive_kernel(
 
         column_bytes = PACK * 2
         feature = [held("feature%d" % t, [P, S], F32) for t in range(PACK)]
-
-        def late_weights():
-            for t in range(EARLY, PACK):
-                weight.append(placed("weight%d" % t, [P, S], F32, 48 + 4 * (t - EARLY)))
-                nc.scalar.activation(
-                    out=weight[t][:], in_=wgs_late[:, t - EARLY, :], func=ACT.Copy, scale=gain_sb[:, t : t + 1]
-                )
-
         for t, cols in pieces:
-            if t < PACK - 1:
-                squares = placed("squares", [P, 32 * KIB // 4], F32, 24)
-            else:
-                late_weights()
-                squares = placed("last_squares", [P, 25 * KIB // 4], F32, 23)[:, KIB // 4 :]
+            squares = placed("squares", [P, 24 * KIB // 4], F32, 24)
             for run in bank_runs(cols):
                 i = runs.index((t, run))
                 if i >= Q_BANKS:

@@ -117,13 +117,13 @@ def tile_list_allergy_archive_kernel(
         identity = held("identity", [P, P], F32)
         make_identity(nc, identity[:])
         spread = placed("spread", [P, HALVES, BLOCKS, PACK, P], F32, 24)
-        for h, copy_out in enumerate((nc.scalar.copy, nc.vector.tensor_copy)):
+        for h in range(HALVES):
             turned = bank(HALVES * (PACK - 1) + h)
             for g in range(BLOCKS):
                 j0 = h * BANK + g * P
                 nc.tensor.transpose(turned[:, g * P : (g + 1) * P], wgs_sb[:, j0 : j0 + P], identity[:])
             by_slice = turned[:].rearrange("p (g i t) -> p g t i", g=BLOCKS, t=PACK)
-            copy_out(
+            nc.scalar.copy(
                 out=spread[:, h].rearrange("p g t (q i) -> p g t q i", i=QUAD),
                 in_=by_slice.unsqueeze(3).to_broadcast([P, BLOCKS, PACK, QUADS, QUAD]),
             )

from contextlib import ExitStack

import concourse.mybir as mybir
from concourse.masks import make_identity

K, T, S, T2, H, N = 1024, 4096, 1024, 2048, 512, 512
FLOPS = 2 * K * H * S + 2 * 2 * H * N * T2

F32 = mybir.dt.float32
BF16 = mybir.dt.bfloat16
I32 = mybir.dt.int32
U32 = mybir.dt.uint32
U16 = mybir.dt.uint16
U8 = mybir.dt.uint8
FP8X4 = mybir.dt.float8_e4m3fn_x4
FP4X4 = mybir.dt.float4_e2m1fn_x4
ACT = mybir.ActivationFunctionType
ALU = mybir.AluOpType

P = 128
KIB = 1024
PACK = 4
QUAD = 32
QUADS = P // QUAD
SCALE_ROWS = 4
TAB_SCALE_ROWS = K // 32
BANK = 512
ROW_STEP = P // TAB_SCALE_ROWS
GROUP = 16
PASSES = K // (P * PACK)
HALVES = S // BANK
BANKS = 8
WIDTHS = (BANK // 2, BANK // 2, BANK, BANK, BANK)
CHUNKS = len(WIDTHS)
BLOCKS = BANK // P
RUN = 4
Q_BANKS = 4
FIRST = 256
VECTOR_CHUNKS = 4
Y_BUFS = 7


def tile_list_allergy_archive_kernel(
    tc, tab_words, tab_scales, offs, w1, gain, page0, offs2, wgs, wa, wb_words, wb_scales,
    out_0, out_1, out_2, out_3,
):
    nc = tc.nc
    with ExitStack() as ctx:
        lists = ctx.enter_context(tc.tile_pool(name="lists", bufs=1))
        keep = ctx.enter_context(tc.tile_pool(name="keep", bufs=1))
        loads = ctx.enter_context(tc.tile_pool(name="loads", bufs=1))
        ring = ctx.enter_context(tc.tile_pool(name="ring", bufs=Y_BUFS))
        psum = ctx.enter_context(tc.psum_pool(name="psum", bufs=1))

        def held(name, shape, dtype, after=None):
            return keep.tile(shape, dtype, name=name, tag=after or name, align_bytes=64)

        def placed(name, shape, dtype, kib):
            return loads.tile(shape, dtype, name=name, offset=int(kib * KIB), align_bytes=64)

        def bank(i):
            return psum.tile([P, BANK], F32, name="bank%d" % i)

        def entries(offsets, cols):
            return offsets[:, cols.start // GROUP : cols.stop // GROUP]

        halves = [slice(h * BANK, (h + 1) * BANK) for h in range(HALVES)]
        chunks = [slice(sum(WIDTHS[:c]), sum(WIDTHS[: c + 1])) for c in range(CHUNKS)]
        page_rows = page0.rearrange("(p t) m -> t p m", t=PACK)

        pick = lists.tile([P, S // GROUP], U16, name="pick")
        place = lists.tile([P, S // GROUP], U16, name="place")
        tab_rows = placed("tab_rows", [P, T], U8, 75)
        picked_plane = held("picked_plane", [P, S], U8)
        nc.vector.memset(tab_rows[:].bitcast(I32), 0)
        nc.vector.memset(picked_plane[:].bitcast(I32), 0)

        wgs_sb = held("wgs_sb", [P, S], F32)
        w1_raw = [held("w1_raw%d" % a, [P, PACK, H], F32) for a in range(PASSES)]
        gain_sb = held("gain_sb", [P, PACK], F32)
        tab = [placed("tab0", [P, T], U32, 4)]

        def load_w1(a):
            rows = w1[a * P * PACK : (a + 1) * P * PACK, :]
            nc.sync.dma_start(out=w1_raw[a][:], in_=rows.rearrange("(p j) c -> p j c", j=PACK))

        def load_tab(a, cols):
            words = tab_words[a].rearrange("p n t -> p (n t)").bitcast(I32)
            nc.sync.dma_start(out=tab[a][:, cols].bitcast(I32), in_=words[:, cols])

        nc.sync.dma_start(out=wgs_sb[:], in_=wgs)
        nc.sync.dma_start(pick[:], offs)
        nc.sync.dma_start(
            out=tab_rows[0:P:ROW_STEP, :].bitcast(I32), in_=tab_scales.rearrange("a q n -> (a q) n").bitcast(I32)
        )
        load_w1(0)
        nc.sync.dma_start(out=gain_sb[:], in_=gain.rearrange("(p t) -> p t", t=PACK))
        nc.sync.dma_start(place[:], offs2)
        load_w1(1)
        load_tab(0, slice(0, T))

        picked_rows = held("picked_rows", [P, S], U8)
        nc.vector.tensor_copy(picked_rows[:], tab_rows[:].indirect(pick[:]))
        tab.append(placed("tab1", [P, T], U32, 60))
        for a in range(PASSES):
            for q in range(QUADS):
                first = ROW_STEP * SCALE_ROWS * (QUADS * a + q)
                to = QUAD * q + SCALE_ROWS * a
                nc.sync.dma_start(
                    out=picked_plane[to : to + SCALE_ROWS, :].bitcast(I32),
                    in_=picked_rows[first : first + ROW_STEP * SCALE_ROWS : ROW_STEP, :].bitcast(I32),
                )
            load_tab(1, slice(a * T // PASSES, (a + 1) * T // PASSES))
        page = [placed("page0", [P, T2], F32, 76)]
        nc.sync.dma_start(out=page[0][:], in_=page_rows[0])

        identity = held("identity", [P, P], F32)
        make_identity(nc, identity[:])
        spread = placed("spread", [P, HALVES, BLOCKS, PACK, P], F32, 24)
        for h in range(HALVES):
            turned = bank(HALVES * (PACK - 1) + h)
            for g in range(BLOCKS):
                j0 = h * BANK + g * P
                nc.tensor.transpose(turned[:, g * P : (g + 1) * P], wgs_sb[:, j0 : j0 + P], identity[:])
            by_slice = turned[:].rearrange("p (g i t) -> p g t i", g=BLOCKS, t=PACK)
            nc.scalar.copy(
                out=spread[:, h].rearrange("p g t (q i) -> p g t q i", i=QUAD),
                in_=by_slice.unsqueeze(3).to_broadcast([P, BLOCKS, PACK, QUADS, QUAD]),
            )
        weight = []
        for t in range(PACK):
            weight.append(held("weight%d" % t, [P, S], F32))
            for h in range(HALVES):
                back = bank(HALVES * t + h)
                for g in range(BLOCKS):
                    nc.tensor.transpose(back[:, g * P : (g + 1) * P], spread[:, h, g, t, :], identity[:])
                out, factor = weight[t][:, halves[h]], gain_sb[:, t : t + 1]
                if t < 2:
                    nc.vector.tensor_scalar(out=out, in0=back[:], scalar1=factor, scalar2=None, op0=ALU.mult)
                else:
                    nc.scalar.activation(out=out, in_=back[:], func=ACT.Copy, scale=factor)

        w1_codes, w1_plane, picked = [], [], []
        for a, engine_copy in enumerate((nc.scalar.copy, nc.vector.tensor_copy)):
            w1_bf = held("w1_bf%d" % a, [P, PACK * H], BF16)
            engine_copy(
                out=w1_bf[:].rearrange("p (t m j) -> p m t j", t=PACK, j=PACK),
                in_=w1_raw[a][:].rearrange("p j (m t) -> p m t j", t=PACK),
            )
            w1_codes.append(held("w1_codes%d" % a, [P, H], U32))
            w1_plane.append(held("w1_plane%d" % a, [P, H], U8))
            nc.vector.quantize_mx(out=w1_codes[a][:].bitcast(FP8X4), scales=w1_plane[a][:], in_=w1_bf[:])

        def gather_words(a):
            picked.append([held("picked%d_%d" % (a, h), [P, BANK], U32) for h in range(HALVES)])
            cuts = halves if a < PASSES - 1 else [slice(0, FIRST), slice(FIRST, BANK), halves[1]]
            for cols in cuts:
                h = cols.start // BANK
                nc.vector.tensor_copy(
                    picked[a][h][:, cols.start - h * BANK : cols.stop - h * BANK], tab[a][:].indirect(entries(pick, cols))
                )

        gather_words(0)
        page.append(placed("page1", [P, T2], F32, 0))
        nc.sync.dma_start(out=page[1][:], in_=page_rows[1])
        wa_raw = placed("wa_raw", [P, PACK * N], F32, 8)
        nc.sync.dma_start(out=wa_raw[:], in_=wa.rearrange("(p j) n -> p (j n)", j=PACK))

        gather_words(1)
        page.append(placed("page2", [P, T2], F32, 56))
        page.append(placed("page3", [P, T2], F32, 66))
        for t in range(2, PACK):
            nc.sync.dma_start(out=page[t][:], in_=page_rows[t])
        wb_codes = placed("wb_codes", [P, 2 * N], U8, 64)
        wb_plane = placed("wb_plane", [P, N], U8, 65)
        nc.sync.dma_start(out=wb_codes[:].bitcast(I32), in_=wb_words[0].bitcast(I32))
        nc.gpsimd.memset(wb_plane[:].bitcast(I32), 0)
        for q in range(QUADS):
            nc.sync.dma_start(
                out=wb_plane[QUAD * q : QUAD * q + SCALE_ROWS, :].bitcast(I32),
                in_=wb_scales[0, SCALE_ROWS * q : SCALE_ROWS * (q + 1), :].bitcast(I32),
            )

        pieces = [(0, slice(0, FIRST)), (1, halves[0]), (0, slice(FIRST, S)), (1, halves[1])]
        pieces.extend((t, slice(0, S)) for t in range(2, PACK))

        def bank_runs(cols):
            if cols.stop == FIRST:
                return [slice(0, FIRST // 2), slice(FIRST // 2, FIRST)]
            return [
                slice(max(cols.start, half.start), min(cols.stop, half.stop))
                for half in halves
                if cols.start < half.stop and half.start < cols.stop
            ]

        runs = [(t, run) for t, cols in pieces for run in bank_runs(cols)]
        q_sum = {}

        def first_stage_pass(a, t, run):
            rows = slice(t * P, (t + 1) * P)
            h = run.start // BANK
            nc.tensor.matmul_mx(
                out=q_sum[t, run.start],
                lhsT=w1_codes[a][:, rows].bitcast(FP8X4),
                lhsT_scale=w1_plane[a][:, rows],
                rhs=picked[a][h][:, run.start - h * BANK : run.stop - h * BANK].bitcast(FP8X4),
                rhs_scale=picked_plane[SCALE_ROWS * a :, run],
                start=(a == 0),
                stop=(a == PASSES - 1),
            )

        for i, (t, run) in enumerate(runs[:Q_BANKS]):
            q_sum[t, run.start] = bank(i)[:, : run.stop - run.start]
            first_stage_pass(0, t, run)

        column_bytes = PACK * 2
        feature = [held("feature%d" % t, [P, S], F32) for t in range(PACK)]
        for t, cols in pieces:
            squares = placed("squares", [P, 24 * KIB // 4], F32, 24)
            for run in bank_runs(cols):
                i = runs.index((t, run))
                if i >= Q_BANKS:
                    q_sum[t, run.start] = bank(i % Q_BANKS)[:, : run.stop - run.start]
                    first_stage_pass(0, t, run)
                first_stage_pass(1, t, run)
                nc.scalar.activation(out=squares[:, run], in_=q_sum[t, run.start], func=ACT.Square)
            for run in bank_runs(cols) if cols.stop == FIRST else [cols]:
                nc.scalar.activation(out=feature[t][:, run], in_=squares[:, run], func=ACT.Exp, scale=-1.0)

        wa_bf = placed("wa_bf", [P, N * PACK], BF16, 28)
        nc.scalar.activation(
            out=wa_bf[:].rearrange("p (c i j) -> p c j i", i=RUN, j=PACK),
            in_=wa_raw[:].rearrange("p (j c i) -> p c j i", i=RUN, j=PACK),
            func=ACT.Copy,
        )

        out_1_rows = out_1.rearrange("(p t) m -> t p m", t=PACK)
        pairs = [
            placed("pairs%d" % c, [P, 2, WIDTHS[c], 2], BF16, 32 + chunks[c].start * column_bytes // KIB)
            for c in range(CHUNKS)
        ]

        def round_into_pairs(t, c):
            nc.scalar.activation(out=pairs[c][:, t // 2, :, t % 2], in_=page[t][:, chunks[c]], func=ACT.Copy)

        for t, cols in pieces:
            nc.vector.tensor_tensor(
                page[t][:].indirect(entries(place, cols)), feature[t][:, cols], weight[t][:, cols], ALU.mult
            )
            if cols.stop == S:
                nc.sync.dma_start(out=out_1_rows[t], in_=page[t][:])
                if t < PACK - 1:
                    for c in range(CHUNKS):
                        round_into_pairs(t, c)

        wa_codes = held("wa_codes", [P, N], U32, after="feature%d" % (PACK - 1))
        wa_plane = held("wa_plane", [P, N], U8)
        nc.vector.quantize_mx(out=wa_codes[:].bitcast(FP8X4), scales=wa_plane[:], in_=wa_bf[:])

        page_plane = held("page_plane", [P, T2], U8)
        out_2_words = out_2[0].rearrange("p m t -> p (m t)").bitcast(I32)
        page_codes = held("page_codes", [P, T2], U32)

        def quantise_chunk(c):
            round_into_pairs(PACK - 1, c)
            grouped = held("grouped%d" % c, [P, WIDTHS[c] * PACK], BF16)
            (nc.vector.tensor_copy if c < VECTOR_CHUNKS else nc.scalar.copy)(
                out=grouped[:].bitcast(U32).rearrange("p (m u) -> p m u", u=2),
                in_=pairs[c][:].rearrange("p u m e -> p (u m e)").bitcast(U32).rearrange("p (u m) -> p m u", u=2),
            )
            nc.vector.quantize_mx(
                out=page_codes[:, chunks[c]].bitcast(FP8X4), scales=page_plane[:, chunks[c]], in_=grouped[:]
            )

        def store_codes(cols):
            nc.sync.dma_start(out=out_2_words[:, cols], in_=page_codes[:, cols].bitcast(I32))

        def store_page_plane():
            for q in range(QUADS):
                nc.gpsimd.dma_start(
                    out=out_3[0, SCALE_ROWS * q : SCALE_ROWS * (q + 1), :].bitcast(I32),
                    in_=page_plane[QUAD * q : QUAD * q + SCALE_ROWS, :].bitcast(I32),
                )

        made = []

        def multiply(n, cols, y):
            rows = slice(n * P, (n + 1) * P)
            first = 2 * len(made) % BANKS
            made.append(y)
            a_sum, b_sum = bank(first), bank(first + 1)
            nc.tensor.matmul_mx(
                out=a_sum[:],
                lhsT=wa_codes[:, rows].bitcast(FP8X4),
                lhsT_scale=wa_plane[:, rows],
                rhs=page_codes[:, cols].bitcast(FP8X4),
                rhs_scale=page_plane[:, cols],
                start=True,
                stop=True,
            )
            nc.tensor.matmul_mx(
                out=b_sum[:],
                lhsT=wb_codes[:, 2 * rows.start : 2 * rows.stop].bitcast(FP4X4),
                lhsT_scale=wb_plane[:, rows],
                rhs=page_codes[:, cols].bitcast(FP8X4),
                rhs_scale=page_plane[:, cols],
                start=True,
                stop=True,
            )
            nc.scalar.activation(out=y, in_=a_sum[:], func=ACT.Tanh)
            nc.vector.tensor_tensor(y, b_sum[:], y, ALU.add)

        def multiply_and_store(n, cols):
            y = ring.tile([P, cols.stop - cols.start], F32, name="y")
            for m0 in range(cols.start, cols.stop, BANK):
                multiply(n, slice(m0, m0 + BANK), y[:, m0 - cols.start : m0 - cols.start + BANK])
            nc.sync.dma_start(out=out_0[n * P : (n + 1) * P, cols], in_=y[:])

        quarters = [slice(m0, m0 + BANK) for m0 in range(0, T2, BANK)]
        page_halves = [slice(m0, m0 + 2 * BANK) for m0 in range(0, T2, 2 * BANK)]
        row_blocks = range(N // P)
        quantise_chunk(0)
        quantise_chunk(1)
        store_codes(quarters[0])
        for c in range(2, CHUNKS):
            quantise_chunk(c)
            store_codes(chunks[c])
        store_page_plane()
        for cols in quarters[:2]:
            multiply_and_store(row_blocks[0], cols)
        for n in row_blocks[1:]:
            multiply_and_store(n, page_halves[0])
        for n in row_blocks[:-1]:
            multiply_and_store(n, page_halves[1])
        for cols in quarters[2:]:
            multiply_and_store(row_blocks[-1], cols)
